import numpy as np
import ml_dtypes


def mxq(x, axis, fmt="e4m3"):
    dtype, down = {"e4m3": (ml_dtypes.float8_e4m3fn, 7), "e5m2": (ml_dtypes.float8_e5m2, 14)}[fmt]
    v = np.moveaxis(np.asarray(x, np.float32).astype(ml_dtypes.bfloat16).astype(np.float64), axis, -1)
    blocks = v.reshape(v.shape[:-1] + (-1, 32))
    amax = np.abs(blocks).max(-1, keepdims=True)
    byte = np.maximum(np.where(amax > 0, np.frexp(amax)[1] - 1 + 127, 0) - down, 1)
    scale = np.exp2(byte - 127.0)
    codes = (blocks / scale).astype(np.float32).astype(dtype).astype(np.float64)
    return np.moveaxis((codes * scale).reshape(v.shape), -1, axis)


WIDE = False


def mx_kscale(k):
    if not WIDE:
        return np.ones(k)
    levels = np.array([10, -10, 5, -5, 0])
    if k % 512:
        return np.exp2(np.random.permutation(np.resize(levels, k // 32))).repeat(32)
    a = np.empty((k // 512, 16))
    for p in range(k // 512):
        a[p, :8] = np.random.permutation(np.resize(levels, 8))
        for g in range(8):
            far = levels[np.abs(levels - a[p, g]) >= 10]
            a[p, g + 8] = far[np.random.randint(len(far))]
    return np.exp2(a.ravel()).repeat(32)


BF16 = ml_dtypes.bfloat16


def bf(x):
    return np.asarray(x, np.float32).astype(BF16)


def f64(x):
    return np.asarray(x).astype(np.float64)

E4M3FN = np.array([(-1.0 if i & 128 else 1.0) * ((1.0 + (i & 7) / 8.0) * 2.0 ** (((i >> 3) & 15) - 7) if i & 120 else (i & 7) * 2.0 ** -9) for i in range(256)])


def e4m3fn_bytes(y):
    return np.clip(np.asarray(y, np.float64), -448.0, 448.0).astype(np.float32).astype(ml_dtypes.float8_e4m3fn).view(np.uint8)


def e4m3fn_values(b):
    return E4M3FN[b]


T, K, N, B = 1024, 2048, 1024, 128


def setup_inputs():
    s = mx_kscale(K)
    mom = np.random.standard_normal((T, K)) * s
    basis = np.random.standard_normal((K, N)) / np.sqrt(K) / s[:, None]
    mom_scale = (np.abs(mom).reshape(T, K // B, B).max(axis=2) / 448.0).astype(np.float32)
    basis_scale = (np.abs(basis).reshape(K // B, B, N // B, B).max(axis=(1, 3)) / 448.0).astype(np.float32)
    return {"mom_bytes": e4m3fn_bytes(mom / np.repeat(f64(mom_scale), B, axis=1)),
            "mom_scale": mom_scale,
            "basis_bytes": e4m3fn_bytes(basis / np.repeat(np.repeat(f64(basis_scale), B, axis=0), B, axis=1)),
            "basis_scale": basis_scale,
            "grad": bf(np.random.standard_normal((T, K)) * s),
            "accum": bf(0.25 + np.random.random((T, N)))}


def reference(mom_bytes, mom_scale, basis_bytes, basis_scale, grad, accum):
    mom = e4m3fn_values(mom_bytes) * np.repeat(f64(mom_scale), B, axis=1)
    basis = e4m3fn_values(basis_bytes) * np.repeat(np.repeat(f64(basis_scale), B, axis=0), B, axis=1)
    bq = mxq(basis, 0, "e4m3")
    r = mxq(mom, 1, "e4m3") @ bq
    h = mxq(f64(grad), 1, "e4m3") @ bq
    new_accum = f64(accum) + h * h
    step = r / np.sqrt(new_accum)
    return step, new_accum

@@ -1,0 +1,297 @@
+from contextlib import ExitStack
+
+import concourse.mybir as mybir
+from concourse.masks import make_identity
+
+T, K, N, B = 1024, 2048, 1024, 128
+FLOPS = 2 * 2 * T * K * N
+
+F32 = mybir.dt.float32
+BF16 = mybir.dt.bfloat16
+U32 = mybir.dt.uint32
+U8 = mybir.dt.uint8
+FP8 = mybir.dt.float8_e4m3fn
+FP8X4 = mybir.dt.float8_e4m3fn_x4
+MULT = mybir.AluOpType.mult
+ADD = mybir.AluOpType.add
+ACT = mybir.ActivationFunctionType
+
+P = 128
+PASSES = K // 512
+TILES = T // P
+HALF = 512
+
+
+def tile_eigenbasis_adagrad_step_d2_kernel(tc, mom_bytes, mom_scale, basis_bytes, basis_scale, grad, accum, out_0, out_1):
+    nc = tc.nc
+    with ExitStack() as ctx:
+        keep = ctx.enter_context(tc.tile_pool(name="keep", bufs=1))
+        work = ctx.enter_context(tc.tile_pool(name="work", bufs=3))
+        tps = ctx.enter_context(tc.psum_pool(name="tps", bufs=4))
+        accs = ctx.enter_context(tc.psum_pool(name="accs", bufs=4))
+
+        mom_rows = mom_bytes.rearrange("(p i) k -> p i k", i=TILES)
+        grad_rows = grad.rearrange("(p i) k -> p i k", i=TILES)
+        accum_rows = accum.rearrange("(p i) n -> p i n", i=TILES)
+        step_rows = out_0.rearrange("(p i) n -> p i n", i=TILES)
+        newacc_rows = out_1.rearrange("(p i) n -> p i n", i=TILES)
+
+        ms = keep.tile([P, TILES, K // B], F32, name="ms")
+        bs = keep.tile([P, PASSES, N // B], F32, name="bs")
+        nc.scalar.dma_start(out=ms[:], in_=mom_scale.rearrange("(p i) j -> p i j", i=TILES))
+        bsv = basis_scale.rearrange("(g q) b -> q g b", q=4)
+        for q in range(4):
+            nc.scalar.dma_start(out=bs[32 * q : 32 * q + 32, :, :], in_=bsv[q].partition_broadcast(32))
+
+        basis_src = basis_bytes.rearrange("(g p t) n -> g p (t n)", p=P, t=4)
+        bb = [keep.tile([P, 4 * N], U8, name="bb%d" % g) for g in range(PASSES)]
+        mb, gr, ac = {}, {}, {}
+
+        def load_m(js):
+            t = keep.tile([P, len(js), K], U8, name="mb%d" % js[0])
+            nc.sync.dma_start(out=t[:], in_=mom_rows[:, js[0] : js[0] + len(js), :])
+            for n, i in enumerate(js):
+                mb[i] = t[:, n, :]
+
+        def load_g(js):
+            t = keep.tile([P, len(js), K], BF16, name="gr%d" % js[0])
+            nc.sync.dma_start(out=t[:], in_=grad_rows[:, js[0] : js[0] + len(js), :])
+            for n, i in enumerate(js):
+                gr[i] = t[:, n, :]
+
+        def load_a(js):
+            t = keep.tile([P, len(js), N], BF16, name="ac%d" % js[0])
+            nc.sync.dma_start(out=t[:], in_=accum_rows[:, js[0] : js[0] + len(js), :])
+            for n, i in enumerate(js):
+                ac[i] = t[:, n, :]
+
+        def load_b(g):
+            nc.sync.dma_start(out=bb[g][:], in_=basis_src[g])
+
+        load_m([0])
+        load_b(0)
+        load_g([0])
+        load_b(1)
+        load_m([1])
+        load_b(2)
+        load_g([1])
+        load_b(3)
+        load_m([2, 3])
+        load_g([2, 3])
+        load_m([4, 5])
+        load_a([0, 1])
+        load_g([4, 5])
+        load_a([2, 3])
+        load_m([6, 7])
+        load_g([6, 7])
+        load_a([4, 5])
+        load_a([6, 7])
+
+        ident = keep.tile([P, P], F32, name="ident")
+        make_identity(nc, ident[:])
+
+        bq, bqs = {}, {}
+        def basis_ready(g, h, widen_on_vector=False):
+            wide = work.tile([P, 4, HALF], BF16, name="bwide", bufs=3)
+            for t in range(4):
+                src = bb[g][:, t * N + h * HALF : t * N + h * HALF + HALF].bitcast(FP8)
+                if widen_on_vector:
+                    nc.vector.tensor_copy(out=wide[:, t, :], in_=src)
+                else:
+                    nc.scalar.copy(out=wide[:, t, :], in_=src)
+            grp = work.tile([P, HALF, 4], BF16, name="bgrp", align_bytes=64, bufs=3)
+            for b in range(4):
+                nc.vector.tensor_scalar(
+                    out=grp[:, 128 * b : 128 * b + 128, :],
+                    in0=wide[:, :, 128 * b : 128 * b + 128].rearrange("p t n -> p n t"),
+                    scalar1=bs[:, g, 4 * h + b : 4 * h + b + 1],
+                    scalar2=None,
+                    op0=MULT,
+                )
+            c = keep.tile([P, HALF], U32, name="bq%d%d" % (g, h), align_bytes=64)
+            s = keep.tile([P, HALF], U8, name="bqs%d%d" % (g, h), align_bytes=64)
+            nc.vector.quantize_mx(out=c[:].bitcast(FP8X4), scales=s[:], in_=grp[:].rearrange("p n t -> p (n t)"))
+            bq[g, h], bqs[g, h] = c, s
+
+        mwide = {}
+        def widen_mom(i, on_scalar=False):
+            w = work.tile([P, PASSES, 2, P, 2], BF16, name="mwide", align_bytes=64, bufs=3)
+            for g in range(PASSES):
+                for q in range(4):
+                    k0 = 512 * g + B * q
+                    nc.vector.tensor_scalar(
+                        out=w[:, g, :, 32 * q : 32 * q + 32, :].rearrange("p u w e -> p w u e"),
+                        in0=mb[i][:, k0 : k0 + B].bitcast(FP8).rearrange("p (w u e) -> p w u e", u=2, e=2),
+                        scalar1=ms[:, i, 4 * g + q : 4 * g + q + 1],
+                        scalar2=None,
+                        op0=MULT,
+                    )
+            mwide[i] = w
+
+        grp_of = {}
+        def turn(kind, i, engines):
+            if kind == "m":
+                words = mwide[i][:].rearrange("p g u w e -> p (g u w e)").bitcast(F32)
+            else:
+                words = gr[i].bitcast(F32)
+            grp = work.tile([P, PASSES, P, 4], BF16, name="grp", align_bytes=64, bufs=6)
+            gw = grp[:].rearrange("p g r t -> p (g r t)").bitcast(F32).rearrange("p (g r u) -> p g r u", r=P, u=2)
+            for half in range(2):
+                bank = tps.tile([P, 2, 2, P], F32, name="tp")
+                for gg in range(2):
+                    for u in range(2):
+                        g = 2 * half + gg
+                        if kind == "m":
+                            src = words[:, (2 * g + u) * P : (2 * g + u + 1) * P]
+                        else:
+                            src = words[:, 256 * g + u : 256 * (g + 1) : 2]
+                        nc.tensor.transpose(bank[:, gg, u, :], src, ident[:])
+                dst = gw[:, 2 * half : 2 * half + 2, :, :]
+                srcb = bank[:].rearrange("p g u r -> p g r u")
+                if engines[half] == "s":
+                    nc.scalar.copy(out=dst, in_=srcb)
+                else:
+                    nc.vector.tensor_copy(out=dst, in_=srcb)
+            grp_of[kind, i] = grp
+
+        xq, xqs = {}, {}
+        def quant(kind, i):
+            c = work.tile([P, PASSES * P], U32, name=kind + "q", align_bytes=64, bufs=8)
+            s = work.tile([P, PASSES * P], U8, name=kind + "qs", align_bytes=64, bufs=8)
+            nc.vector.quantize_mx(out=c[:].bitcast(FP8X4), scales=s[:], in_=grp_of[kind, i][:].rearrange("p g r t -> p (g r t)"))
+            xq[kind, i], xqs[kind, i] = c, s
+
+        acc = {}
+        def mx_pass(kind, i, h, g):
+            if g == 0:
+                acc[kind, i, h] = accs.tile([P, HALF], F32, name="acc")
+            nc.tensor.matmul_mx(
+                out=acc[kind, i, h][:],
+                lhsT=xq[kind, i][:, g * P : (g + 1) * P].bitcast(FP8X4),
+                lhsT_scale=xqs[kind, i][:, g * P : (g + 1) * P],
+                rhs=bq[g, h][:].bitcast(FP8X4),
+                rhs_scale=bqs[g, h][:],
+                start=(g == 0),
+                stop=(g == PASSES - 1),
+            )
+
+        def mx(kind, i, h):
+            for g in range(PASSES):
+                mx_pass(kind, i, h, g)
+
+        def finish(i, h):
+            sq = work.tile([P, HALF], F32, name="sq", bufs=3)
+            nc.scalar.activation(out=sq[:], in_=acc["g", i, h][:], func=ACT.Square)
+            na = work.tile([P, HALF], F32, name="na", bufs=4)
+            cols = slice(h * HALF, h * HALF + HALF)
+            nc.vector.tensor_tensor(out=na[:], in0=sq[:], in1=ac[i][:, cols], op=ADD)
+            rs = work.tile([P, HALF], F32, name="rs", bufs=3)
+            nc.scalar.activation(out=rs[:], in_=na[:], func=ACT.Abs_reciprocal_sqrt)
+            st = work.tile([P, HALF], F32, name="st", bufs=4)
+            nc.vector.tensor_tensor(out=st[:], in0=acc["m", i, h][:], in1=rs[:], op=MULT)
+            nc.sync.dma_start(out=newacc_rows[:, i, cols], in_=na[:])
+            nc.sync.dma_start(out=step_rows[:, i, cols], in_=st[:])
+
+        def prep(i):
+            widen_mom(i)
+            turn("g", i, "ss")
+            turn("m", i, "ss")
+            quant("g", i)
+            quant("m", i)
+
+        turn("g", 3, "ss")
+        quant("g", 3)
+        turn("g", 1, "ss")
+        quant("g", 1)
+        widen_mom(0)
+        turn("m", 0, "vs")
+        quant("m", 0)
+        basis_ready(0, 0)
+        basis_ready(1, 0)
+        turn("g", 0, "ss")
+        quant("g", 0)
+        widen_mom(2)
+        widen_mom(3)
+        basis_ready(3, 0, widen_on_vector=True)
+        turn("g", 5, "ss")
+        quant("g", 5)
+        basis_ready(2, 0, widen_on_vector=True)
+        widen_mom(5)
+        mx("g", 0, 0)
+        mx("m", 0, 0)
+        finish(0, 0)
+        turn("m", 2, "ss")
+        quant("m", 2)
+        turn("g", 7, "vs")
+        quant("g", 7)
+        turn("g", 2, "ss")
+        quant("g", 2)
+        turn("m", 3, "ss")
+        quant("m", 3)
+        mx("g", 2, 0)
+        mx("m", 2, 0)
+        finish(2, 0)
+        mx("g", 3, 0)
+        mx("m", 3, 0)
+        finish(3, 0)
+        widen_mom(4)
+        turn("g", 6, "ss")
+        quant("g", 6)
+        basis_ready(2, 1)
+        turn("g", 4, "ss")
+        quant("g", 4)
+        basis_ready(1, 1)
+        basis_ready(0, 1, widen_on_vector=True)
+        turn("m", 5, "ss")
+        quant("m", 5)
+        basis_ready(3, 1)
+        mx("g", 5, 0)
+        mx("m", 5, 0)
+        finish(5, 0)
+        mx("g", 5, 1)
+        mx("m", 5, 1)
+        finish(5, 1)
+        widen_mom(7)
+        mx("g", 2, 1)
+        mx("m", 2, 1)
+        finish(2, 1)
+        turn("m", 4, "vs")
+        quant("m", 4)
+        mx("g", 4, 1)
+        mx("m", 4, 1)
+        finish(4, 1)
+        widen_mom(1)
+        widen_mom(6)
+        mx("g", 0, 1)
+        mx("m", 0, 1)
+        finish(0, 1)
+        mx("g", 3, 1)
+        mx("m", 3, 1)
+        finish(3, 1)
+        turn("m", 7, "ss")
+        quant("m", 7)
+        turn("m", 1, "vs")
+        quant("m", 1)
+        mx("g", 7, 0)
+        mx("m", 7, 0)
+        finish(7, 0)
+        turn("m", 6, "vs")
+        quant("m", 6)
+        mx("g", 7, 1)
+        mx("m", 7, 1)
+        finish(7, 1)
+        mx("g", 1, 1)
+        mx("m", 1, 1)
+        finish(1, 1)
+        mx("g", 6, 0)
+        mx("m", 6, 0)
+        finish(6, 0)
+        mx("g", 6, 1)
+        mx("m", 6, 1)
+        finish(6, 1)
+        mx("g", 4, 0)
+        mx("m", 4, 0)
+        finish(4, 0)
+        mx("g", 1, 0)
+        mx("m", 1, 0)
+        finish(1, 0)

@@ -19,7 +19,8 @@ ACT = mybir.ActivationFunctionType
 P = 128
 PASSES = K // 512
 TILES = T // P
-HALF = 512
+BANK = 512
+PANELS = ((0, 512), (512, 256), (768, 256))
 
 
 def tile_eigenbasis_adagrad_step_d2_kernel(tc, mom_bytes, mom_scale, basis_bytes, basis_scale, grad, accum, out_0, out_1):
@@ -27,271 +28,265 @@ def tile_eigenbasis_adagrad_step_d2_kernel(tc, mom_bytes, mom_scale, basis_bytes
     with ExitStack() as ctx:
         keep = ctx.enter_context(tc.tile_pool(name="keep", bufs=1))
         work = ctx.enter_context(tc.tile_pool(name="work", bufs=3))
-        tps = ctx.enter_context(tc.psum_pool(name="tps", bufs=4))
-        accs = ctx.enter_context(tc.psum_pool(name="accs", bufs=4))
+        turn_ps = ctx.enter_context(tc.psum_pool(name="turn_ps", bufs=4))
+        h_ps = ctx.enter_context(tc.psum_pool(name="h_ps", bufs=2))
+        r_ps = ctx.enter_context(tc.psum_pool(name="r_ps", bufs=2))
+        ctx.enter_context(tc.manual_schedule())
 
         mom_rows = mom_bytes.rearrange("(p i) k -> p i k", i=TILES)
         grad_rows = grad.rearrange("(p i) k -> p i k", i=TILES)
         accum_rows = accum.rearrange("(p i) n -> p i n", i=TILES)
         step_rows = out_0.rearrange("(p i) n -> p i n", i=TILES)
         newacc_rows = out_1.rearrange("(p i) n -> p i n", i=TILES)
+        basis_rows = basis_bytes.rearrange("(g p t) n -> g p t n", p=P, t=4)
 
-        ms = keep.tile([P, TILES, K // B], F32, name="ms")
-        bs = keep.tile([P, PASSES, N // B], F32, name="bs")
-        nc.scalar.dma_start(out=ms[:], in_=mom_scale.rearrange("(p i) j -> p i j", i=TILES))
-        bsv = basis_scale.rearrange("(g q) b -> q g b", q=4)
+        mom_sc = keep.tile([P, TILES, K // B], F32, name="mom_sc")
+        basis_sc = keep.tile([P, PASSES, N // B], F32, name="basis_sc")
+        nc.scalar.dma_start(out=mom_sc[:], in_=mom_scale.rearrange("(p i) j -> p i j", i=TILES))
+        all_sc = keep.tile([P, PASSES, 4, N // B], F32, name="all_sc")
+        nc.scalar.dma_start(out=all_sc[:].rearrange("p g q b -> p (g q b)"), in_=basis_scale.rearrange("j b -> (j b)").partition_broadcast(P))
         for q in range(4):
-            nc.scalar.dma_start(out=bs[32 * q : 32 * q + 32, :, :], in_=bsv[q].partition_broadcast(32))
+            nc.vector.tensor_copy(out=basis_sc[32 * q : 32 * q + 32, :, :], in_=all_sc[32 * q : 32 * q + 32, :, q, :])
 
-        basis_src = basis_bytes.rearrange("(g p t) n -> g p (t n)", p=P, t=4)
-        bb = [keep.tile([P, 4 * N], U8, name="bb%d" % g) for g in range(PASSES)]
-        mb, gr, ac = {}, {}, {}
+        basis_raw, mom_raw, grad_raw, accum_raw = {}, {}, {}, {}
 
-        def load_m(js):
-            t = keep.tile([P, len(js), K], U8, name="mb%d" % js[0])
-            nc.sync.dma_start(out=t[:], in_=mom_rows[:, js[0] : js[0] + len(js), :])
-            for n, i in enumerate(js):
-                mb[i] = t[:, n, :]
+        def load_basis(c, g):
+            n0, w = PANELS[c]
+            basis_raw[c, g] = keep.tile([P, 4, w], U8, name="basis_raw%d%d" % (c, g))
+            nc.sync.dma_start(out=basis_raw[c, g][:], in_=basis_rows[g][:, :, n0 : n0 + w])
 
-        def load_g(js):
-            t = keep.tile([P, len(js), K], BF16, name="gr%d" % js[0])
-            nc.sync.dma_start(out=t[:], in_=grad_rows[:, js[0] : js[0] + len(js), :])
-            for n, i in enumerate(js):
-                gr[i] = t[:, n, :]
+        def load_mom(i):
+            mom_raw[i] = keep.tile([P, K], U8, name="mom_raw%d" % i)
+            nc.sync.dma_start(out=mom_raw[i][:], in_=mom_rows[:, i, :])
 
-        def load_a(js):
-            t = keep.tile([P, len(js), N], BF16, name="ac%d" % js[0])
-            nc.sync.dma_start(out=t[:], in_=accum_rows[:, js[0] : js[0] + len(js), :])
-            for n, i in enumerate(js):
-                ac[i] = t[:, n, :]
+        def load_grad(i):
+            grad_raw[i] = keep.tile([P, K], BF16, name="grad_raw%d" % i)
+            nc.sync.dma_start(out=grad_raw[i][:], in_=grad_rows[:, i, :])
 
-        def load_b(g):
-            nc.sync.dma_start(out=bb[g][:], in_=basis_src[g])
+        def load_accum(j):
+            accum_raw[j] = keep.tile([P, 2, N], BF16, name="accum_raw%d" % j)
+            nc.sync.dma_start(out=accum_raw[j][:], in_=accum_rows[:, 2 * j : 2 * j + 2, :])
 
-        load_m([0])
-        load_b(0)
-        load_g([0])
-        load_b(1)
-        load_m([1])
-        load_b(2)
-        load_g([1])
-        load_b(3)
-        load_m([2, 3])
-        load_g([2, 3])
-        load_m([4, 5])
-        load_a([0, 1])
-        load_g([4, 5])
-        load_a([2, 3])
-        load_m([6, 7])
-        load_g([6, 7])
-        load_a([4, 5])
-        load_a([6, 7])
+        load_basis(0, 0)
+        load_mom(0)
+        load_grad(0)
+        load_basis(0, 1)
+        load_basis(0, 2)
+        load_basis(0, 3)
+        load_grad(1)
+        for i in range(1, TILES):
+            load_mom(i)
+            if i + 1 < TILES:
+                load_grad(i + 1)
+            if i % 2 == 1:
+                load_accum(i // 2)
+                load_basis(1, i // 2)
+        for g in range(PASSES):
+            load_basis(2, g)
 
         ident = keep.tile([P, P], F32, name="ident")
         make_identity(nc, ident[:])
 
-        bq, bqs = {}, {}
-        def basis_ready(g, h, widen_on_vector=False):
-            wide = work.tile([P, 4, HALF], BF16, name="bwide", bufs=3)
-            for t in range(4):
-                src = bb[g][:, t * N + h * HALF : t * N + h * HALF + HALF].bitcast(FP8)
-                if widen_on_vector:
-                    nc.vector.tensor_copy(out=wide[:, t, :], in_=src)
-                else:
-                    nc.scalar.copy(out=wide[:, t, :], in_=src)
-            grp = work.tile([P, HALF, 4], BF16, name="bgrp", align_bytes=64, bufs=3)
-            for b in range(4):
+        basis_wide, basis_grp, basis_q, basis_qs = {}, {}, {}, {}
+
+        def basis_widen(c, g, t0, t1):
+            w = PANELS[c][1]
+            if t0 == 0:
+                basis_wide[c, g] = work.tile([P, 4, w], BF16, name="basis_wide", bufs=3)
+            nc.scalar.copy(out=basis_wide[c, g][:, t0:t1, :], in_=basis_raw[c, g][:, t0:t1, :].bitcast(FP8))
+
+        def basis_interleave(c, g):
+            n0, w = PANELS[c]
+            grp = work.tile([P, w, 4], BF16, name="basis_grp", align_bytes=64, bufs=3)
+            for b in range(w // B):
+                cols = slice(B * b, B * b + B)
                 nc.vector.tensor_scalar(
-                    out=grp[:, 128 * b : 128 * b + 128, :],
-                    in0=wide[:, :, 128 * b : 128 * b + 128].rearrange("p t n -> p n t"),
-                    scalar1=bs[:, g, 4 * h + b : 4 * h + b + 1],
+                    out=grp[:, cols, :].rearrange("p (c i) t -> p c t i", i=4),
+                    in0=basis_wide[c, g][:, :, cols].rearrange("p t (c i) -> p c t i", i=4),
+                    scalar1=basis_sc[:, g, n0 // B + b : n0 // B + b + 1],
                     scalar2=None,
                     op0=MULT,
                 )
-            c = keep.tile([P, HALF], U32, name="bq%d%d" % (g, h), align_bytes=64)
-            s = keep.tile([P, HALF], U8, name="bqs%d%d" % (g, h), align_bytes=64)
-            nc.vector.quantize_mx(out=c[:].bitcast(FP8X4), scales=s[:], in_=grp[:].rearrange("p n t -> p (n t)"))
-            bq[g, h], bqs[g, h] = c, s
+            basis_grp[c, g] = grp
 
-        mwide = {}
-        def widen_mom(i, on_scalar=False):
-            w = work.tile([P, PASSES, 2, P, 2], BF16, name="mwide", align_bytes=64, bufs=3)
+        def basis_quant(c, g):
+            w = PANELS[c][1]
+            basis_q[c, g] = keep.tile([P, w], U32, name="basis_q%d%d" % (c, g), align_bytes=64)
+            basis_qs[c, g] = keep.tile([P, w], U8, name="basis_qs%d%d" % (c, g), align_bytes=64)
+            nc.vector.quantize_mx(out=basis_q[c, g][:].bitcast(FP8X4), scales=basis_qs[c, g][:], in_=basis_grp[c, g][:].rearrange("p n t -> p (n t)"))
+
+        mom_wide, turned, grouped, codes, scales = {}, {}, {}, {}, {}
+
+        def mom_widen(i):
+            w = work.tile([P, PASSES, 2, P, 2], BF16, name="mom_wide", align_bytes=64, bufs=3)
             for g in range(PASSES):
                 for q in range(4):
                     k0 = 512 * g + B * q
                     nc.vector.tensor_scalar(
                         out=w[:, g, :, 32 * q : 32 * q + 32, :].rearrange("p u w e -> p w u e"),
-                        in0=mb[i][:, k0 : k0 + B].bitcast(FP8).rearrange("p (w u e) -> p w u e", u=2, e=2),
-                        scalar1=ms[:, i, 4 * g + q : 4 * g + q + 1],
+                        in0=mom_raw[i][:, k0 : k0 + B].bitcast(FP8).rearrange("p (w u e) -> p w u e", u=2, e=2),
+                        scalar1=mom_sc[:, i, 4 * g + q : 4 * g + q + 1],
                         scalar2=None,
                         op0=MULT,
                     )
-            mwide[i] = w
+            mom_wide[i] = w
 
-        grp_of = {}
-        def turn(kind, i, engines):
-            if kind == "m":
-                words = mwide[i][:].rearrange("p g u w e -> p (g u w e)").bitcast(F32)
+        def turn(kind, i):
+            if kind == "mom":
+                words = mom_wide[i][:].rearrange("p g u w e -> p (g u w e)").bitcast(F32)
             else:
-                words = gr[i].bitcast(F32)
-            grp = work.tile([P, PASSES, P, 4], BF16, name="grp", align_bytes=64, bufs=6)
-            gw = grp[:].rearrange("p g r t -> p (g r t)").bitcast(F32).rearrange("p (g r u) -> p g r u", r=P, u=2)
+                words = grad_raw[i][:].bitcast(F32)
             for half in range(2):
-                bank = tps.tile([P, 2, 2, P], F32, name="tp")
+                bank = turn_ps.tile([P, 2, 2, P], F32, name="turn")
                 for gg in range(2):
                     for u in range(2):
                         g = 2 * half + gg
-                        if kind == "m":
+                        if kind == "mom":
                             src = words[:, (2 * g + u) * P : (2 * g + u + 1) * P]
                         else:
                             src = words[:, 256 * g + u : 256 * (g + 1) : 2]
                         nc.tensor.transpose(bank[:, gg, u, :], src, ident[:])
-                dst = gw[:, 2 * half : 2 * half + 2, :, :]
-                srcb = bank[:].rearrange("p g u r -> p g r u")
-                if engines[half] == "s":
-                    nc.scalar.copy(out=dst, in_=srcb)
-                else:
-                    nc.vector.tensor_copy(out=dst, in_=srcb)
-            grp_of[kind, i] = grp
+                turned[kind, i, half] = bank
 
-        xq, xqs = {}, {}
+        def unload(kind, i, half):
+            if half == 0:
+                grouped[kind, i] = work.tile([P, PASSES, P, 4], BF16, name="grouped", align_bytes=64, bufs=4)
+            words = grouped[kind, i][:].rearrange("p g r t -> p (g r t)").bitcast(F32).rearrange("p (g r u) -> p g r u", r=P, u=2)
+            nc.scalar.copy(out=words[:, 2 * half : 2 * half + 2, :, :], in_=turned[kind, i, half][:].rearrange("p g u r -> p g r u"))
+
         def quant(kind, i):
-            c = work.tile([P, PASSES * P], U32, name=kind + "q", align_bytes=64, bufs=8)
-            s = work.tile([P, PASSES * P], U8, name=kind + "qs", align_bytes=64, bufs=8)
-            nc.vector.quantize_mx(out=c[:].bitcast(FP8X4), scales=s[:], in_=grp_of[kind, i][:].rearrange("p g r t -> p (g r t)"))
-            xq[kind, i], xqs[kind, i] = c, s
+            codes[kind, i] = keep.tile([P, PASSES * P], U32, name="%s_q%d" % (kind, i), align_bytes=64)
+            scales[kind, i] = keep.tile([P, PASSES * P], U8, name="%s_qs%d" % (kind, i), align_bytes=64)
+            nc.vector.quantize_mx(out=codes[kind, i][:].bitcast(FP8X4), scales=scales[kind, i][:], in_=grouped[kind, i][:].rearrange("p g r t -> p (g r t)"))
 
-        acc = {}
-        def mx_pass(kind, i, h, g):
-            if g == 0:
-                acc[kind, i, h] = accs.tile([P, HALF], F32, name="acc")
+        units = [(c, i, BANK // w) for c, (n0, w) in enumerate(PANELS) for i in range(0, TILES, BANK // w)]
+        sums, square, newacc, root = {}, {}, {}, {}
+
+        def mx_pass(kind, s, j, g):
+            c, i, n = units[s]
+            if j == 0 and g == 0:
+                pool = h_ps if kind == "grad" else r_ps
+                sums[kind, s] = pool.tile([P, n, PANELS[c][1]], F32, name="sums")
             nc.tensor.matmul_mx(
-                out=acc[kind, i, h][:],
-                lhsT=xq[kind, i][:, g * P : (g + 1) * P].bitcast(FP8X4),
-                lhsT_scale=xqs[kind, i][:, g * P : (g + 1) * P],
-                rhs=bq[g, h][:].bitcast(FP8X4),
-                rhs_scale=bqs[g, h][:],
+                out=sums[kind, s][:, j, :],
+                lhsT=codes[kind, i + j][:, g * P : (g + 1) * P].bitcast(FP8X4),
+                lhsT_scale=scales[kind, i + j][:, g * P : (g + 1) * P],
+                rhs=basis_q[c, g][:].bitcast(FP8X4),
+                rhs_scale=basis_qs[c, g][:],
                 start=(g == 0),
                 stop=(g == PASSES - 1),
             )
 
-        def mx(kind, i, h):
-            for g in range(PASSES):
-                mx_pass(kind, i, h, g)
+        def mx(kind, s):
+            for j in range(units[s][2]):
+                for g in range(PASSES):
+                    mx_pass(kind, s, j, g)
 
-        def finish(i, h):
-            sq = work.tile([P, HALF], F32, name="sq", bufs=3)
-            nc.scalar.activation(out=sq[:], in_=acc["g", i, h][:], func=ACT.Square)
-            na = work.tile([P, HALF], F32, name="na", bufs=4)
-            cols = slice(h * HALF, h * HALF + HALF)
-            nc.vector.tensor_tensor(out=na[:], in0=sq[:], in1=ac[i][:, cols], op=ADD)
-            rs = work.tile([P, HALF], F32, name="rs", bufs=3)
-            nc.scalar.activation(out=rs[:], in_=na[:], func=ACT.Abs_reciprocal_sqrt)
-            st = work.tile([P, HALF], F32, name="st", bufs=4)
-            nc.vector.tensor_tensor(out=st[:], in0=acc["m", i, h][:], in1=rs[:], op=MULT)
-            nc.sync.dma_start(out=newacc_rows[:, i, cols], in_=na[:])
-            nc.sync.dma_start(out=step_rows[:, i, cols], in_=st[:])
+        def out_view(rows, s):
+            c, i, n = units[s]
+            n0, w = PANELS[c]
+            return rows[:, i : i + n, n0 : n0 + w]
 
-        def prep(i):
-            widen_mom(i)
-            turn("g", i, "ss")
-            turn("m", i, "ss")
-            quant("g", i)
-            quant("m", i)
+        def do_square(s):
+            c, i, n = units[s]
+            square[s] = work.tile([P, n, PANELS[c][1]], F32, name="square", bufs=2)
+            nc.scalar.activation(out=square[s][:], in_=sums["grad", s][:], func=ACT.Square)
 
-        turn("g", 3, "ss")
-        quant("g", 3)
-        turn("g", 1, "ss")
-        quant("g", 1)
-        widen_mom(0)
-        turn("m", 0, "vs")
-        quant("m", 0)
-        basis_ready(0, 0)
-        basis_ready(1, 0)
-        turn("g", 0, "ss")
-        quant("g", 0)
-        widen_mom(2)
-        widen_mom(3)
-        basis_ready(3, 0, widen_on_vector=True)
-        turn("g", 5, "ss")
-        quant("g", 5)
-        basis_ready(2, 0, widen_on_vector=True)
-        widen_mom(5)
-        mx("g", 0, 0)
-        mx("m", 0, 0)
-        finish(0, 0)
-        turn("m", 2, "ss")
-        quant("m", 2)
-        turn("g", 7, "vs")
-        quant("g", 7)
-        turn("g", 2, "ss")
-        quant("g", 2)
-        turn("m", 3, "ss")
-        quant("m", 3)
-        mx("g", 2, 0)
-        mx("m", 2, 0)
-        finish(2, 0)
-        mx("g", 3, 0)
-        mx("m", 3, 0)
-        finish(3, 0)
-        widen_mom(4)
-        turn("g", 6, "ss")
-        quant("g", 6)
-        basis_ready(2, 1)
-        turn("g", 4, "ss")
-        quant("g", 4)
-        basis_ready(1, 1)
-        basis_ready(0, 1, widen_on_vector=True)
-        turn("m", 5, "ss")
-        quant("m", 5)
-        basis_ready(3, 1)
-        mx("g", 5, 0)
-        mx("m", 5, 0)
-        finish(5, 0)
-        mx("g", 5, 1)
-        mx("m", 5, 1)
-        finish(5, 1)
-        widen_mom(7)
-        mx("g", 2, 1)
-        mx("m", 2, 1)
-        finish(2, 1)
-        turn("m", 4, "vs")
-        quant("m", 4)
-        mx("g", 4, 1)
-        mx("m", 4, 1)
-        finish(4, 1)
-        widen_mom(1)
-        widen_mom(6)
-        mx("g", 0, 1)
-        mx("m", 0, 1)
-        finish(0, 1)
-        mx("g", 3, 1)
-        mx("m", 3, 1)
-        finish(3, 1)
-        turn("m", 7, "ss")
-        quant("m", 7)
-        turn("m", 1, "vs")
-        quant("m", 1)
-        mx("g", 7, 0)
-        mx("m", 7, 0)
-        finish(7, 0)
-        turn("m", 6, "vs")
-        quant("m", 6)
-        mx("g", 7, 1)
-        mx("m", 7, 1)
-        finish(7, 1)
-        mx("g", 1, 1)
-        mx("m", 1, 1)
-        finish(1, 1)
-        mx("g", 6, 0)
-        mx("m", 6, 0)
-        finish(6, 0)
-        mx("g", 6, 1)
-        mx("m", 6, 1)
-        finish(6, 1)
-        mx("g", 4, 0)
-        mx("m", 4, 0)
-        finish(4, 0)
-        mx("g", 1, 0)
-        mx("m", 1, 0)
-        finish(1, 0)
+        def do_add(s):
+            c, i, n = units[s]
+            n0, w = PANELS[c]
+            newacc[s] = work.tile([P, n, w], F32, name="newacc", bufs=5)
+            nc.vector.tensor_tensor(out=newacc[s][:], in0=square[s][:], in1=accum_raw[i // 2][:, i % 2 : i % 2 + n, n0 : n0 + w], op=ADD)
+            nc.sync.dma_start(out=out_view(newacc_rows, s), in_=newacc[s][:])
+
+        def do_root(s):
+            c, i, n = units[s]
+            root[s] = work.tile([P, n, PANELS[c][1]], F32, name="root", bufs=3)
+            nc.scalar.activation(out=root[s][:], in_=newacc[s][:], func=ACT.Abs_reciprocal_sqrt)
+
+        def do_step(s):
+            c, i, n = units[s]
+            st = work.tile([P, n, PANELS[c][1]], F32, name="step", bufs=5)
+            nc.vector.tensor_tensor(out=st[:], in0=sums["mom", s][:], in1=root[s][:], op=MULT)
+            nc.sync.dma_start(out=out_view(step_rows, s), in_=st[:])
+
+        basis_widen(0, 0, 0, 2)
+        basis_widen(0, 0, 2, 4)
+        mom_widen(0)
+        turn("grad", 0)
+        turn("mom", 0)
+        basis_interleave(0, 0)
+        basis_widen(0, 1, 0, 4)
+        unload("grad", 0, 0)
+        unload("grad", 0, 1)
+        turn("grad", 1)
+        basis_quant(0, 0)
+        basis_interleave(0, 1)
+        quant("grad", 0)
+        basis_quant(0, 1)
+        mx_pass("grad", 0, 0, 0)
+        mx_pass("grad", 0, 0, 1)
+        basis_widen(0, 2, 0, 4)
+        mom_widen(1)
+        basis_interleave(0, 2)
+        basis_widen(0, 3, 0, 4)
+        unload("mom", 0, 0)
+        unload("mom", 0, 1)
+        unload("grad", 1, 0)
+        unload("grad", 1, 1)
+        basis_quant(0, 2)
+        mx_pass("grad", 0, 0, 2)
+        basis_interleave(0, 3)
+        quant("mom", 0)
+        basis_quant(0, 3)
+        quant("grad", 1)
+
+        later = [(c, g, t) for c in (1, 2) for g in range(PASSES) for t in (0, 2)]
+        widened = 0
+        for s in range(len(units)):
+            if s + 2 < TILES:
+                turn("grad", s + 2)
+            if s + 1 < TILES:
+                turn("mom", s + 1)
+            if 0 < s < TILES:
+                quant("mom", s)
+            if s == 0:
+                mx_pass("grad", 0, 0, 3)
+            else:
+                do_add(s)
+            if s + 1 < len(units):
+                mx("grad", s + 1)
+            mx("mom", s)
+
+            ready = []
+            for c, g, t in later[widened : widened + (1 if s + 2 < TILES else 2)]:
+                basis_widen(c, g, t, t + 2)
+                widened = widened + 1
+                if t == 2:
+                    ready.append((c, g))
+            if s + 2 < TILES:
+                unload("grad", s + 2, 0)
+                unload("grad", s + 2, 1)
+                mom_widen(s + 2)
+            if s == 0:
+                do_square(0)
+            else:
+                do_root(s)
+            for c, g in ready:
+                basis_interleave(c, g)
+            if s > 0:
+                do_step(s - 1)
+            if s + 2 < TILES:
+                quant("grad", s + 2)
+            for c, g in ready:
+                basis_quant(c, g)
+            if s == 0:
+                do_add(0)
+            if s + 1 < TILES:
+                unload("mom", s + 1, 0)
+                unload("mom", s + 1, 1)
+            if s == 0:
+                do_root(0)
+            if s + 1 < len(units):
+                do_square(s + 1)
+        do_step(len(units) - 1)

@@ -20,6 +20,7 @@ P = 128
 PASSES = K // 512
 TILES = T // P
 BANK = 512
+ON_SCALAR = (1, 7)
 PANELS = ((0, 512), (512, 256), (768, 256))
 
 
@@ -28,9 +29,7 @@ def tile_eigenbasis_adagrad_step_d2_kernel(tc, mom_bytes, mom_scale, basis_bytes
     with ExitStack() as ctx:
         keep = ctx.enter_context(tc.tile_pool(name="keep", bufs=1))
         work = ctx.enter_context(tc.tile_pool(name="work", bufs=3))
-        turn_ps = ctx.enter_context(tc.psum_pool(name="turn_ps", bufs=4))
-        h_ps = ctx.enter_context(tc.psum_pool(name="h_ps", bufs=2))
-        r_ps = ctx.enter_context(tc.psum_pool(name="r_ps", bufs=2))
+        psum = ctx.enter_context(tc.psum_pool(name="psum", bufs=1))
         ctx.enter_context(tc.manual_schedule())
 
         mom_rows = mom_bytes.rearrange("(p i) k -> p i k", i=TILES)
@@ -45,10 +44,14 @@ def tile_eigenbasis_adagrad_step_d2_kernel(tc, mom_bytes, mom_scale, basis_bytes
         nc.scalar.dma_start(out=mom_sc[:], in_=mom_scale.rearrange("(p i) j -> p i j", i=TILES))
         all_sc = keep.tile([P, PASSES, 4, N // B], F32, name="all_sc")
         nc.scalar.dma_start(out=all_sc[:].rearrange("p g q b -> p (g q b)"), in_=basis_scale.rearrange("j b -> (j b)").partition_broadcast(P))
+        warm = keep.tile([P, 2], F32, name="warm")
+        nc.vector.memset(warm[:, 0:1], 1.0)
+        nc.scalar.activation(out=warm[:, 1:2], in_=warm[:, 0:1], func=ACT.Abs_reciprocal_sqrt)
         for q in range(4):
             nc.vector.tensor_copy(out=basis_sc[32 * q : 32 * q + 32, :, :], in_=all_sc[32 * q : 32 * q + 32, :, q, :])
 
-        basis_raw, mom_raw, grad_raw, accum_raw = {}, {}, {}, {}
+        basis_raw, mom_raw, grad_raw = {}, {}, {}
+        accum_raw = keep.tile([P, TILES, N], BF16, name="accum_raw")
 
         def load_basis(c, g):
             n0, w = PANELS[c]
@@ -64,36 +67,37 @@ def tile_eigenbasis_adagrad_step_d2_kernel(tc, mom_bytes, mom_scale, basis_bytes
             nc.sync.dma_start(out=grad_raw[i][:], in_=grad_rows[:, i, :])
 
         def load_accum(j):
-            accum_raw[j] = keep.tile([P, 2, N], BF16, name="accum_raw%d" % j)
-            nc.sync.dma_start(out=accum_raw[j][:], in_=accum_rows[:, 2 * j : 2 * j + 2, :])
+            nc.sync.dma_start(out=accum_raw[:, 2 * j : 2 * j + 2, :], in_=accum_rows[:, 2 * j : 2 * j + 2, :])
 
         load_basis(0, 0)
-        load_mom(0)
-        load_grad(0)
         load_basis(0, 1)
+        load_grad(0)
+        load_mom(0)
         load_basis(0, 2)
         load_basis(0, 3)
         load_grad(1)
         for i in range(1, TILES):
-            load_mom(i)
+            load_mom((0, 1, 2, 7, 3, 4, 5, 6)[i])
             if i + 1 < TILES:
                 load_grad(i + 1)
             if i % 2 == 1:
                 load_accum(i // 2)
                 load_basis(1, i // 2)
-        for g in range(PASSES):
-            load_basis(2, g)
+        for c in range(2, len(PANELS)):
+            for g in range(PASSES):
+                load_basis(c, g)
 
         ident = keep.tile([P, P], F32, name="ident")
         make_identity(nc, ident[:])
 
         basis_wide, basis_grp, basis_q, basis_qs = {}, {}, {}, {}
 
-        def basis_widen(c, g, t0, t1):
+        def basis_widen(c, g, t0, t1, on_vector=False):
             w = PANELS[c][1]
             if t0 == 0:
                 basis_wide[c, g] = work.tile([P, 4, w], BF16, name="basis_wide", bufs=3)
-            nc.scalar.copy(out=basis_wide[c, g][:, t0:t1, :], in_=basis_raw[c, g][:, t0:t1, :].bitcast(FP8))
+            copy = nc.vector.tensor_copy if on_vector else nc.scalar.copy
+            copy(out=basis_wide[c, g][:, t0:t1, :], in_=basis_raw[c, g][:, t0:t1, :].bitcast(FP8))
 
         def basis_interleave(c, g):
             n0, w = PANELS[c]
@@ -131,17 +135,28 @@ def tile_eigenbasis_adagrad_step_d2_kernel(tc, mom_bytes, mom_scale, basis_bytes
                     )
             mom_wide[i] = w
 
+        def mom_widen_scalar(i, j0, j1, on_vector=False):
+            if j0 == 0:
+                mom_wide[i] = work.tile([P, PASSES, 2, P, 2], BF16, name="mom_plain", align_bytes=64, bufs=2)
+            for j in range(j0, j1):
+                dst = mom_wide[i][:].rearrange("p g u w e -> p (g u w e)")[:, B * j : B * j + B]
+                src = mom_raw[i][:, B * j : B * j + B].bitcast(FP8)
+                if on_vector:
+                    nc.vector.tensor_scalar(out=dst, in0=src, scalar1=mom_sc[:, i, j : j + 1], scalar2=None, op0=MULT)
+                else:
+                    nc.scalar.activation(out=dst, in_=src, func=ACT.Copy, scale=mom_sc[:, i, j : j + 1])
+
         def turn(kind, i):
             if kind == "mom":
                 words = mom_wide[i][:].rearrange("p g u w e -> p (g u w e)").bitcast(F32)
             else:
                 words = grad_raw[i][:].bitcast(F32)
             for half in range(2):
-                bank = turn_ps.tile([P, 2, 2, P], F32, name="turn")
+                bank = psum.tile([P, 2, 2, P], F32, name="bank%d" % (len(turned) % 4))
                 for gg in range(2):
                     for u in range(2):
                         g = 2 * half + gg
-                        if kind == "mom":
+                        if kind == "mom" and i not in ON_SCALAR:
                             src = words[:, (2 * g + u) * P : (2 * g + u + 1) * P]
                         else:
                             src = words[:, 256 * g + u : 256 * (g + 1) : 2]
@@ -165,8 +180,10 @@ def tile_eigenbasis_adagrad_step_d2_kernel(tc, mom_bytes, mom_scale, basis_bytes
         def mx_pass(kind, s, j, g):
             c, i, n = units[s]
             if j == 0 and g == 0:
-                pool = h_ps if kind == "grad" else r_ps
-                sums[kind, s] = pool.tile([P, n, PANELS[c][1]], F32, name="sums")
+                own = (4, 5) if kind == "grad" else (6, 7)
+                freed = (0, 1) if kind == "grad" else (2, 3)
+                bank = own[s % 2] if s < TILES else (freed + own)[s % 4]
+                sums[kind, s] = psum.tile([P, n, PANELS[c][1]], F32, name="bank%d" % bank)
             nc.tensor.matmul_mx(
                 out=sums[kind, s][:, j, :],
                 lhsT=codes[kind, i + j][:, g * P : (g + 1) * P].bitcast(FP8X4),
@@ -196,7 +213,7 @@ def tile_eigenbasis_adagrad_step_d2_kernel(tc, mom_bytes, mom_scale, basis_bytes
             c, i, n = units[s]
             n0, w = PANELS[c]
             newacc[s] = work.tile([P, n, w], F32, name="newacc", bufs=5)
-            nc.vector.tensor_tensor(out=newacc[s][:], in0=square[s][:], in1=accum_raw[i // 2][:, i % 2 : i % 2 + n, n0 : n0 + w], op=ADD)
+            nc.vector.tensor_tensor(out=newacc[s][:], in0=square[s][:], in1=accum_raw[:, i : i + n, n0 : n0 + w], op=ADD)
             nc.sync.dma_start(out=out_view(newacc_rows, s), in_=newacc[s][:])
 
         def do_root(s):
@@ -211,82 +228,109 @@ def tile_eigenbasis_adagrad_step_d2_kernel(tc, mom_bytes, mom_scale, basis_bytes
             nc.sync.dma_start(out=out_view(step_rows, s), in_=st[:])
 
         basis_widen(0, 0, 0, 2)
-        basis_widen(0, 0, 2, 4)
-        mom_widen(0)
-        turn("grad", 0)
-        turn("mom", 0)
-        basis_interleave(0, 0)
+        basis_widen(0, 0, 2, 4, True)
         basis_widen(0, 1, 0, 4)
+        basis_interleave(0, 0)
+        turn("grad", 0)
+        mom_widen(0)
+        turn("mom", 0)
         unload("grad", 0, 0)
+        basis_widen(0, 2, 0, 4)
         unload("grad", 0, 1)
         turn("grad", 1)
         basis_quant(0, 0)
         basis_interleave(0, 1)
+        basis_interleave(0, 2)
         quant("grad", 0)
         basis_quant(0, 1)
+        basis_quant(0, 2)
         mx_pass("grad", 0, 0, 0)
         mx_pass("grad", 0, 0, 1)
-        basis_widen(0, 2, 0, 4)
-        mom_widen(1)
-        basis_interleave(0, 2)
+        mx_pass("grad", 0, 0, 2)
         basis_widen(0, 3, 0, 4)
         unload("mom", 0, 0)
         unload("mom", 0, 1)
+        turn("grad", 2)
         unload("grad", 1, 0)
         unload("grad", 1, 1)
-        basis_quant(0, 2)
-        mx_pass("grad", 0, 0, 2)
+        mom_widen_scalar(1, 0, 8)
         basis_interleave(0, 3)
         quant("mom", 0)
+        mx_pass("mom", 0, 0, 0)
+        mx_pass("mom", 0, 0, 1)
+        mx_pass("mom", 0, 0, 2)
         basis_quant(0, 3)
+        mx_pass("grad", 0, 0, 3)
+        mx_pass("mom", 0, 0, 3)
         quant("grad", 1)
+        unload("grad", 2, 0)
+        unload("grad", 2, 1)
+        mom_widen_scalar(1, 8, 16)
+        quant("grad", 2)
 
-        later = [(c, g, t) for c in (1, 2) for g in range(PASSES) for t in (0, 2)]
-        widened = 0
+        later = [(c, g, t, t + BANK // w) for c, (n0, w) in enumerate(PANELS) if c > 0 for g in range(PASSES) for t in range(0, 4, BANK // w)]
+        quota = [1,1,1,1,1,1,2,2,2,2,2] + [0] * 16
+        epi = [1] + [1] * 16
+        share = [0,3,3,3,3] + [0] * 16
+        widened, e, shared = 0, 0, 0
         for s in range(len(units)):
-            if s + 2 < TILES:
+            if 0 < s < TILES - 2:
                 turn("grad", s + 2)
             if s + 1 < TILES:
                 turn("mom", s + 1)
             if 0 < s < TILES:
                 quant("mom", s)
-            if s == 0:
-                mx_pass("grad", 0, 0, 3)
-            else:
-                do_add(s)
+            if s > 0 and epi[s] > 0:
+                do_add(e)
             if s + 1 < len(units):
                 mx("grad", s + 1)
-            mx("mom", s)
+            if s > 0:
+                mx("mom", s)
 
             ready = []
-            for c, g, t in later[widened : widened + (1 if s + 2 < TILES else 2)]:
-                basis_widen(c, g, t, t + 2)
+            for c, g, t0, t1 in later[widened : widened + quota[s]]:
+                basis_widen(c, g, t0, t1)
                 widened = widened + 1
-                if t == 2:
+                if t1 == 4:
                     ready.append((c, g))
-            if s + 2 < TILES:
+            if 0 < s < TILES - 2:
                 unload("grad", s + 2, 0)
                 unload("grad", s + 2, 1)
+            if s + 2 < TILES and s + 2 not in ON_SCALAR:
                 mom_widen(s + 2)
+            if s + 2 == 7 and shared + share[s] < 16:
+                mom_widen_scalar(7, shared + share[s], 16, True)
             if s == 0:
                 do_square(0)
-            else:
-                do_root(s)
+            if s + 1 < TILES:
+                unload("mom", s + 1, 0)
+                unload("mom", s + 1, 1)
+            if s > 0 and epi[s] > 0:
+                do_root(e)
+            if share[s] > 0:
+                mom_widen_scalar(7, shared, shared + share[s])
+                shared = shared + share[s]
             for c, g in ready:
                 basis_interleave(c, g)
-            if s > 0:
-                do_step(s - 1)
-            if s + 2 < TILES:
+            if s > 0 and epi[s] > 0:
+                do_step(e - 1)
+            if 0 < s < TILES - 2:
                 quant("grad", s + 2)
             for c, g in ready:
                 basis_quant(c, g)
             if s == 0:
                 do_add(0)
-            if s + 1 < TILES:
-                unload("mom", s + 1, 0)
-                unload("mom", s + 1, 1)
             if s == 0:
                 do_root(0)
-            if s + 1 < len(units):
-                do_square(s + 1)
+            if epi[s] > 0:
+                e = e + 1
+                if e < len(units):
+                    do_square(e)
+            if epi[s] > 1:
+                do_add(e)
+                do_step(e - 1)
+                do_root(e)
+                e = e + 1
+                if e < len(units):
+                    do_square(e)
         do_step(len(units) - 1)

@@ -20,7 +20,6 @@ P = 128
 PASSES = K // 512
 TILES = T // P
 BANK = 512
-ON_SCALAR = (1, 7)
 PANELS = ((0, 512), (512, 256), (768, 256))
 
 
@@ -56,7 +55,8 @@ def tile_eigenbasis_adagrad_step_d2_kernel(tc, mom_bytes, mom_scale, basis_bytes
         def load_basis(c, g):
             n0, w = PANELS[c]
             basis_raw[c, g] = keep.tile([P, 4, w], U8, name="basis_raw%d%d" % (c, g))
-            nc.sync.dma_start(out=basis_raw[c, g][:], in_=basis_rows[g][:, :, n0 : n0 + w])
+            for t0, t1 in ((0, 2), (2, 4)) if (c, g) == (0, 0) else ((0, 4),):
+                nc.sync.dma_start(out=basis_raw[c, g][:, t0:t1, :], in_=basis_rows[g][:, t0:t1, n0 : n0 + w])
 
         def load_mom(i):
             mom_raw[i] = keep.tile([P, K], U8, name="mom_raw%d" % i)
@@ -120,31 +120,26 @@ def tile_eigenbasis_adagrad_step_d2_kernel(tc, mom_bytes, mom_scale, basis_bytes
             nc.vector.quantize_mx(out=basis_q[c, g][:].bitcast(FP8X4), scales=basis_qs[c, g][:], in_=basis_grp[c, g][:].rearrange("p n t -> p (n t)"))
 
         mom_wide, turned, grouped, codes, scales = {}, {}, {}, {}, {}
+        plain = set()
 
-        def mom_widen(i):
-            w = work.tile([P, PASSES, 2, P, 2], BF16, name="mom_wide", align_bytes=64, bufs=3)
-            for g in range(PASSES):
-                for q in range(4):
-                    k0 = 512 * g + B * q
+        def mom_widen(i, j0=0, j1=K // B, on_scalar=False):
+            if i not in mom_wide:
+                mom_wide[i] = work.tile([P, PASSES, 2, P, 2], BF16, name="mom_wide", align_bytes=64, bufs=4)
+            for j in range(j0, j1):
+                g, q = divmod(j, 4)
+                src = mom_raw[i][:, B * j : B * j + B].bitcast(FP8)
+                if on_scalar:
+                    plain.add((i, g))
+                    dst = mom_wide[i][:].rearrange("p g u w e -> p (g u w e)")[:, B * j : B * j + B]
+                    nc.scalar.activation(out=dst, in_=src, func=ACT.Copy, scale=mom_sc[:, i, j : j + 1])
+                else:
                     nc.vector.tensor_scalar(
-                        out=w[:, g, :, 32 * q : 32 * q + 32, :].rearrange("p u w e -> p w u e"),
-                        in0=mom_raw[i][:, k0 : k0 + B].bitcast(FP8).rearrange("p (w u e) -> p w u e", u=2, e=2),
-                        scalar1=mom_sc[:, i, 4 * g + q : 4 * g + q + 1],
+                        out=mom_wide[i][:, g, :, 32 * q : 32 * q + 32, :].rearrange("p u w e -> p w u e"),
+                        in0=src.rearrange("p (w u e) -> p w u e", u=2, e=2),
+                        scalar1=mom_sc[:, i, j : j + 1],
                         scalar2=None,
                         op0=MULT,
                     )
-            mom_wide[i] = w
-
-        def mom_widen_scalar(i, j0, j1, on_vector=False):
-            if j0 == 0:
-                mom_wide[i] = work.tile([P, PASSES, 2, P, 2], BF16, name="mom_plain", align_bytes=64, bufs=2)
-            for j in range(j0, j1):
-                dst = mom_wide[i][:].rearrange("p g u w e -> p (g u w e)")[:, B * j : B * j + B]
-                src = mom_raw[i][:, B * j : B * j + B].bitcast(FP8)
-                if on_vector:
-                    nc.vector.tensor_scalar(out=dst, in0=src, scalar1=mom_sc[:, i, j : j + 1], scalar2=None, op0=MULT)
-                else:
-                    nc.scalar.activation(out=dst, in_=src, func=ACT.Copy, scale=mom_sc[:, i, j : j + 1])
 
         def turn(kind, i):
             if kind == "mom":
@@ -156,18 +151,19 @@ def tile_eigenbasis_adagrad_step_d2_kernel(tc, mom_bytes, mom_scale, basis_bytes
                 for gg in range(2):
                     for u in range(2):
                         g = 2 * half + gg
-                        if kind == "mom" and i not in ON_SCALAR:
+                        if kind == "mom" and (i, g) not in plain:
                             src = words[:, (2 * g + u) * P : (2 * g + u + 1) * P]
                         else:
                             src = words[:, 256 * g + u : 256 * (g + 1) : 2]
                         nc.tensor.transpose(bank[:, gg, u, :], src, ident[:])
                 turned[kind, i, half] = bank
 
-        def unload(kind, i, half):
+        def unload(kind, i, half, on_vector=False):
             if half == 0:
                 grouped[kind, i] = work.tile([P, PASSES, P, 4], BF16, name="grouped", align_bytes=64, bufs=4)
             words = grouped[kind, i][:].rearrange("p g r t -> p (g r t)").bitcast(F32).rearrange("p (g r u) -> p g r u", r=P, u=2)
-            nc.scalar.copy(out=words[:, 2 * half : 2 * half + 2, :, :], in_=turned[kind, i, half][:].rearrange("p g u r -> p g r u"))
+            copy = nc.vector.tensor_copy if on_vector else nc.scalar.copy
+            copy(out=words[:, 2 * half : 2 * half + 2, :, :], in_=turned[kind, i, half][:].rearrange("p g u r -> p g r u"))
 
         def quant(kind, i):
             codes[kind, i] = keep.tile([P, PASSES * P], U32, name="%s_q%d" % (kind, i), align_bytes=64)
@@ -176,16 +172,19 @@ def tile_eigenbasis_adagrad_step_d2_kernel(tc, mom_bytes, mom_scale, basis_bytes
 
         units = [(c, i, BANK // w) for c, (n0, w) in enumerate(PANELS) for i in range(0, TILES, BANK // w)]
         sums, square, newacc, root = {}, {}, {}, {}
+        split = ("mom", len(units) - 1)
 
         def mx_pass(kind, s, j, g):
             c, i, n = units[s]
-            if j == 0 and g == 0:
+            if g == 0 and (j == 0 or (kind, s) == split):
                 own = (4, 5) if kind == "grad" else (6, 7)
                 freed = (0, 1) if kind == "grad" else (2, 3)
-                bank = own[s % 2] if s < TILES else (freed + own)[s % 4]
-                sums[kind, s] = psum.tile([P, n, PANELS[c][1]], F32, name="bank%d" % bank)
+                bank = own[s % 2] if s < TILES else (freed + own)[(s + j) % 4]
+                sums[kind, s, j] = psum.tile([P, n, PANELS[c][1]], F32, name="bank%d" % bank)
+                for jj in range(j + 1, n):
+                    sums[kind, s, jj] = sums[kind, s, j]
             nc.tensor.matmul_mx(
-                out=sums[kind, s][:, j, :],
+                out=sums[kind, s, j][:, j, :],
                 lhsT=codes[kind, i + j][:, g * P : (g + 1) * P].bitcast(FP8X4),
                 lhsT_scale=scales[kind, i + j][:, g * P : (g + 1) * P],
                 rhs=basis_q[c, g][:].bitcast(FP8X4),
@@ -207,7 +206,7 @@ def tile_eigenbasis_adagrad_step_d2_kernel(tc, mom_bytes, mom_scale, basis_bytes
         def do_square(s):
             c, i, n = units[s]
             square[s] = work.tile([P, n, PANELS[c][1]], F32, name="square", bufs=2)
-            nc.scalar.activation(out=square[s][:], in_=sums["grad", s][:], func=ACT.Square)
+            nc.scalar.activation(out=square[s][:], in_=sums["grad", s, 0][:], func=ACT.Square)
 
         def do_add(s):
             c, i, n = units[s]
@@ -223,9 +222,10 @@ def tile_eigenbasis_adagrad_step_d2_kernel(tc, mom_bytes, mom_scale, basis_bytes
 
         def do_step(s):
             c, i, n = units[s]
-            st = work.tile([P, n, PANELS[c][1]], F32, name="step", bufs=5)
-            nc.vector.tensor_tensor(out=st[:], in0=sums["mom", s][:], in1=root[s][:], op=MULT)
-            nc.sync.dma_start(out=out_view(step_rows, s), in_=st[:])
+            for js in [slice(j, j + 1) for j in range(n)] if ("mom", s) == split else [slice(0, n)]:
+                st = work.tile([P, js.stop - js.start, PANELS[c][1]], F32, name="step", bufs=5)
+                nc.vector.tensor_tensor(out=st[:], in0=sums["mom", s, js.start][:, js, :], in1=root[s][:, js, :], op=MULT)
+                nc.sync.dma_start(out=out_view(step_rows, s)[:, js, :], in_=st[:])
 
         basis_widen(0, 0, 0, 2)
         basis_widen(0, 0, 2, 4, True)
@@ -253,7 +253,9 @@ def tile_eigenbasis_adagrad_step_d2_kernel(tc, mom_bytes, mom_scale, basis_bytes
         turn("grad", 2)
         unload("grad", 1, 0)
         unload("grad", 1, 1)
-        mom_widen_scalar(1, 0, 8)
+        unload("grad", 2, 0)
+        unload("grad", 2, 1)
+        mom_widen(1, 0, 8, True)
         basis_interleave(0, 3)
         quant("mom", 0)
         mx_pass("mom", 0, 0, 0)
@@ -263,16 +265,13 @@ def tile_eigenbasis_adagrad_step_d2_kernel(tc, mom_bytes, mom_scale, basis_bytes
         mx_pass("grad", 0, 0, 3)
         mx_pass("mom", 0, 0, 3)
         quant("grad", 1)
-        unload("grad", 2, 0)
-        unload("grad", 2, 1)
-        mom_widen_scalar(1, 8, 16)
+        mom_widen(1, 8, 16, False)
         quant("grad", 2)
 
         later = [(c, g, t, t + BANK // w) for c, (n0, w) in enumerate(PANELS) if c > 0 for g in range(PASSES) for t in range(0, 4, BANK // w)]
-        quota = [1,1,1,1,1,1,2,2,2,2,2] + [0] * 16
-        epi = [1] + [1] * 16
-        share = [0,3,3,3,3] + [0] * 16
-        widened, e, shared = 0, 0, 0
+        quota = [1,1,1,1,1,1,2,3,3,2] + [0] * 16
+        share = [0,2,2,2,2] + [0] * 16
+        widened, shared = 0, 0
         for s in range(len(units)):
             if 0 < s < TILES - 2:
                 turn("grad", s + 2)
@@ -280,8 +279,8 @@ def tile_eigenbasis_adagrad_step_d2_kernel(tc, mom_bytes, mom_scale, basis_bytes
                 turn("mom", s + 1)
             if 0 < s < TILES:
                 quant("mom", s)
-            if s > 0 and epi[s] > 0:
-                do_add(e)
+            if s > 0:
+                do_add(s)
             if s + 1 < len(units):
                 mx("grad", s + 1)
             if s > 0:
@@ -296,24 +295,24 @@ def tile_eigenbasis_adagrad_step_d2_kernel(tc, mom_bytes, mom_scale, basis_bytes
             if 0 < s < TILES - 2:
                 unload("grad", s + 2, 0)
                 unload("grad", s + 2, 1)
-            if s + 2 < TILES and s + 2 not in ON_SCALAR:
-                mom_widen(s + 2)
-            if s + 2 == 7 and shared + share[s] < 16:
-                mom_widen_scalar(7, shared + share[s], 16, True)
+            if s + 2 < TILES:
+                mom_widen(s + 2, sum(share) if s + 2 == 7 else 0)
             if s == 0:
                 do_square(0)
             if s + 1 < TILES:
                 unload("mom", s + 1, 0)
                 unload("mom", s + 1, 1)
-            if s > 0 and epi[s] > 0:
-                do_root(e)
+            if s >= TILES - 1 and s + 1 < len(units):
+                do_square(s + 1)
+            if s > 0:
+                do_root(s)
             if share[s] > 0:
-                mom_widen_scalar(7, shared, shared + share[s])
+                mom_widen(7, shared, shared + share[s], True)
                 shared = shared + share[s]
             for c, g in ready:
                 basis_interleave(c, g)
-            if s > 0 and epi[s] > 0:
-                do_step(e - 1)
+            if s > 0:
+                do_step(s - 1)
             if 0 < s < TILES - 2:
                 quant("grad", s + 2)
             for c, g in ready:
@@ -322,15 +321,6 @@ def tile_eigenbasis_adagrad_step_d2_kernel(tc, mom_bytes, mom_scale, basis_bytes
                 do_add(0)
             if s == 0:
                 do_root(0)
-            if epi[s] > 0:
-                e = e + 1
-                if e < len(units):
-                    do_square(e)
-            if epi[s] > 1:
-                do_add(e)
-                do_step(e - 1)
-                do_root(e)
-                e = e + 1
-                if e < len(units):
-                    do_square(e)
+            if s < TILES - 1:
+                do_square(s + 1)
         do_step(len(units) - 1)

@@ -141,12 +141,12 @@ def tile_eigenbasis_adagrad_step_d2_kernel(tc, mom_bytes, mom_scale, basis_bytes
                         op0=MULT,
                     )
 
-        def turn(kind, i):
+        def turn(kind, i, halves=(0, 1)):
             if kind == "mom":
                 words = mom_wide[i][:].rearrange("p g u w e -> p (g u w e)").bitcast(F32)
             else:
                 words = grad_raw[i][:].bitcast(F32)
-            for half in range(2):
+            for half in halves:
                 bank = psum.tile([P, 2, 2, P], F32, name="bank%d" % (len(turned) % 4))
                 for gg in range(2):
                     for u in range(2):
@@ -160,7 +160,7 @@ def tile_eigenbasis_adagrad_step_d2_kernel(tc, mom_bytes, mom_scale, basis_bytes
 
         def unload(kind, i, half, on_vector=False):
             if half == 0:
-                grouped[kind, i] = work.tile([P, PASSES, P, 4], BF16, name="grouped", align_bytes=64, bufs=4)
+                grouped[kind, i] = work.tile([P, PASSES, P, 4], BF16, name="grouped", align_bytes=64, bufs=5)
             words = grouped[kind, i][:].rearrange("p g r t -> p (g r t)").bitcast(F32).rearrange("p (g r u) -> p g r u", r=P, u=2)
             copy = nc.vector.tensor_copy if on_vector else nc.scalar.copy
             copy(out=words[:, 2 * half : 2 * half + 2, :, :], in_=turned[kind, i, half][:].rearrange("p g u r -> p g r u"))
@@ -270,19 +270,22 @@ def tile_eigenbasis_adagrad_step_d2_kernel(tc, mom_bytes, mom_scale, basis_bytes
 
         later = [(c, g, t, t + BANK // w) for c, (n0, w) in enumerate(PANELS) if c > 0 for g in range(PASSES) for t in range(0, 4, BANK // w)]
         quota = [1,1,1,1,1,1,2,3,3,2] + [0] * 16
-        share = [0,2,2,2,2] + [0] * 16
+        share = [0,1,1,1,1] + [0] * 16
         widened, shared = 0, 0
+        last = len(units) - 1
         for s in range(len(units)):
             if 0 < s < TILES - 2:
                 turn("grad", s + 2)
-            if s + 1 < TILES:
-                turn("mom", s + 1)
-            if 0 < s < TILES:
-                quant("mom", s)
             if s > 0:
                 do_add(s)
-            if s + 1 < len(units):
+            if 0 < s < TILES:
+                quant("mom", s)
+            if s + 1 < last:
                 mx("grad", s + 1)
+            if s + 2 == last:
+                mx("grad", last)
+            if s + 1 < TILES:
+                turn("mom", s + 1)
             if s > 0:
                 mx("mom", s)
 
@@ -295,32 +298,31 @@ def tile_eigenbasis_adagrad_step_d2_kernel(tc, mom_bytes, mom_scale, basis_bytes
             if 0 < s < TILES - 2:
                 unload("grad", s + 2, 0)
                 unload("grad", s + 2, 1)
+            if s > 0:
+                do_step(s - 1)
             if s + 2 < TILES:
                 mom_widen(s + 2, sum(share) if s + 2 == 7 else 0)
             if s == 0:
                 do_square(0)
-            if s + 1 < TILES:
-                unload("mom", s + 1, 0)
-                unload("mom", s + 1, 1)
-            if s >= TILES - 1 and s + 1 < len(units):
-                do_square(s + 1)
-            if s > 0:
+                do_add(0)
+            if 0 < s < TILES - 1:
                 do_root(s)
-            if share[s] > 0:
-                mom_widen(7, shared, shared + share[s], True)
-                shared = shared + share[s]
+            if s < last:
+                do_square(s + 1)
+            if s >= TILES - 1:
+                do_root(s)
             for c, g in ready:
                 basis_interleave(c, g)
-            if s > 0:
-                do_step(s - 1)
             if 0 < s < TILES - 2:
                 quant("grad", s + 2)
             for c, g in ready:
                 basis_quant(c, g)
-            if s == 0:
-                do_add(0)
+            if s + 1 < TILES:
+                unload("mom", s + 1, 0)
+                unload("mom", s + 1, 1)
             if s == 0:
                 do_root(0)
-            if s < TILES - 1:
-                do_square(s + 1)
-        do_step(len(units) - 1)
+            if share[s] > 0:
+                mom_widen(7, shared, shared + share[s], True)
+                shared = shared + share[s]
+        do_step(last)

@@ -147,7 +147,8 @@ def tile_eigenbasis_adagrad_step_d2_kernel(tc, mom_bytes, mom_scale, basis_bytes
             else:
                 words = grad_raw[i][:].bitcast(F32)
             for half in halves:
-                bank = psum.tile([P, 2, 2, P], F32, name="bank%d" % (len(turned) % 4))
+                turns = len(turned) // 2
+                bank = psum.tile([P, 2, 2, P], F32, name="bank%d" % (2 * (turns % 2) + (half + turns // 2) % 2))
                 for gg in range(2):
                     for u in range(2):
                         g = 2 * half + gg

@@ -21,6 +21,8 @@ PASSES = K // 512
 TILES = T // P
 BANK = 512
 PANELS = ((0, 512), (512, 256), (768, 256))
+GRAD_LEAD = 3
+HALF_PASSES = (1, 1, 1, 1, 1, 1, 2, 3, 3, 2)
 
 
 def tile_eigenbasis_adagrad_step_d2_kernel(tc, mom_bytes, mom_scale, basis_bytes, basis_scale, grad, accum, out_0, out_1):
@@ -77,41 +79,37 @@ def tile_eigenbasis_adagrad_step_d2_kernel(tc, mom_bytes, mom_scale, basis_bytes
         load_basis(0, 3)
         load_grad(1)
         for i in range(1, TILES):
-            load_mom((0, 1, 2, 7, 3, 4, 5, 6)[i])
+            load_mom(i)
             if i + 1 < TILES:
                 load_grad(i + 1)
             if i % 2 == 1:
                 load_accum(i // 2)
                 load_basis(1, i // 2)
-        for c in range(2, len(PANELS)):
-            for g in range(PASSES):
-                load_basis(c, g)
+        for g in range(PASSES):
+            load_basis(2, g)
 
         ident = keep.tile([P, P], F32, name="ident")
         make_identity(nc, ident[:])
 
         basis_wide, basis_grp, basis_q, basis_qs = {}, {}, {}, {}
 
-        def basis_widen(c, g, t0, t1, on_vector=False):
-            w = PANELS[c][1]
+        def basis_widen(c, g, t0, t1, copy=nc.scalar.copy):
             if t0 == 0:
-                basis_wide[c, g] = work.tile([P, 4, w], BF16, name="basis_wide", bufs=3)
-            copy = nc.vector.tensor_copy if on_vector else nc.scalar.copy
+                basis_wide[c, g] = work.tile([P, 4, PANELS[c][1]], BF16, name="basis_wide", bufs=3)
             copy(out=basis_wide[c, g][:, t0:t1, :], in_=basis_raw[c, g][:, t0:t1, :].bitcast(FP8))
 
         def basis_interleave(c, g):
             n0, w = PANELS[c]
-            grp = work.tile([P, w, 4], BF16, name="basis_grp", align_bytes=64, bufs=3)
+            basis_grp[c, g] = work.tile([P, w, 4], BF16, name="basis_grp", align_bytes=64, bufs=3)
             for b in range(w // B):
                 cols = slice(B * b, B * b + B)
                 nc.vector.tensor_scalar(
-                    out=grp[:, cols, :].rearrange("p (c i) t -> p c t i", i=4),
+                    out=basis_grp[c, g][:, cols, :].rearrange("p (c i) t -> p c t i", i=4),
                     in0=basis_wide[c, g][:, :, cols].rearrange("p t (c i) -> p c t i", i=4),
                     scalar1=basis_sc[:, g, n0 // B + b : n0 // B + b + 1],
                     scalar2=None,
                     op0=MULT,
                 )
-            basis_grp[c, g] = grp
 
         def basis_quant(c, g):
             w = PANELS[c][1]
@@ -120,51 +118,49 @@ def tile_eigenbasis_adagrad_step_d2_kernel(tc, mom_bytes, mom_scale, basis_bytes
             nc.vector.quantize_mx(out=basis_q[c, g][:].bitcast(FP8X4), scales=basis_qs[c, g][:], in_=basis_grp[c, g][:].rearrange("p n t -> p (n t)"))
 
         mom_wide, turned, grouped, codes, scales = {}, {}, {}, {}, {}
-        plain = set()
 
-        def mom_widen(i, j0=0, j1=K // B, on_scalar=False):
+        def mom_widen(i, passes, on_scalar=False):
             if i not in mom_wide:
                 mom_wide[i] = work.tile([P, PASSES, 2, P, 2], BF16, name="mom_wide", align_bytes=64, bufs=4)
-            for j in range(j0, j1):
-                g, q = divmod(j, 4)
-                src = mom_raw[i][:, B * j : B * j + B].bitcast(FP8)
-                if on_scalar:
-                    plain.add((i, g))
-                    dst = mom_wide[i][:].rearrange("p g u w e -> p (g u w e)")[:, B * j : B * j + B]
-                    nc.scalar.activation(out=dst, in_=src, func=ACT.Copy, scale=mom_sc[:, i, j : j + 1])
-                else:
-                    nc.vector.tensor_scalar(
-                        out=mom_wide[i][:, g, :, 32 * q : 32 * q + 32, :].rearrange("p u w e -> p w u e"),
-                        in0=src.rearrange("p (w u e) -> p w u e", u=2, e=2),
-                        scalar1=mom_sc[:, i, j : j + 1],
-                        scalar2=None,
-                        op0=MULT,
-                    )
+            for g in passes:
+                for q in range(4):
+                    j = 4 * g + q
+                    src = mom_raw[i][:, B * j : B * j + B].bitcast(FP8)
+                    if on_scalar:
+                        dst = mom_wide[i][:].rearrange("p g u w e -> p (g u w e)")[:, B * j : B * j + B]
+                        nc.scalar.activation(out=dst, in_=src, func=ACT.Copy, scale=mom_sc[:, i, j : j + 1])
+                    else:
+                        nc.vector.tensor_scalar(
+                            out=mom_wide[i][:, g, :, 32 * q : 32 * q + 32, :].rearrange("p u w e -> p w u e"),
+                            in0=src.rearrange("p (w u e) -> p w u e", u=2, e=2),
+                            scalar1=mom_sc[:, i, j : j + 1],
+                            scalar2=None,
+                            op0=MULT,
+                        )
 
-        def turn(kind, i, halves=(0, 1)):
+        def turn(kind, i):
             if kind == "mom":
                 words = mom_wide[i][:].rearrange("p g u w e -> p (g u w e)").bitcast(F32)
             else:
                 words = grad_raw[i][:].bitcast(F32)
-            for half in halves:
-                turns = len(turned) // 2
+            turns = len(turned) // 2
+            for half in range(2):
                 bank = psum.tile([P, 2, 2, P], F32, name="bank%d" % (2 * (turns % 2) + (half + turns // 2) % 2))
                 for gg in range(2):
                     for u in range(2):
                         g = 2 * half + gg
-                        if kind == "mom" and (i, g) not in plain:
+                        if kind == "mom" and (i, g) != scalar_pass:
                             src = words[:, (2 * g + u) * P : (2 * g + u + 1) * P]
                         else:
                             src = words[:, 256 * g + u : 256 * (g + 1) : 2]
                         nc.tensor.transpose(bank[:, gg, u, :], src, ident[:])
                 turned[kind, i, half] = bank
 
-        def unload(kind, i, half, on_vector=False):
-            if half == 0:
-                grouped[kind, i] = work.tile([P, PASSES, P, 4], BF16, name="grouped", align_bytes=64, bufs=5)
+        def unload(kind, i):
+            grouped[kind, i] = work.tile([P, PASSES, P, 4], BF16, name="grouped", align_bytes=64, bufs=5)
             words = grouped[kind, i][:].rearrange("p g r t -> p (g r t)").bitcast(F32).rearrange("p (g r u) -> p g r u", r=P, u=2)
-            copy = nc.vector.tensor_copy if on_vector else nc.scalar.copy
-            copy(out=words[:, 2 * half : 2 * half + 2, :, :], in_=turned[kind, i, half][:].rearrange("p g u r -> p g r u"))
+            for half in range(2):
+                nc.scalar.copy(out=words[:, 2 * half : 2 * half + 2, :, :], in_=turned[kind, i, half][:].rearrange("p g u r -> p g r u"))
 
         def quant(kind, i):
             codes[kind, i] = keep.tile([P, PASSES * P], U32, name="%s_q%d" % (kind, i), align_bytes=64)
@@ -172,18 +168,18 @@ def tile_eigenbasis_adagrad_step_d2_kernel(tc, mom_bytes, mom_scale, basis_bytes
             nc.vector.quantize_mx(out=codes[kind, i][:].bitcast(FP8X4), scales=scales[kind, i][:], in_=grouped[kind, i][:].rearrange("p g r t -> p (g r t)"))
 
         units = [(c, i, BANK // w) for c, (n0, w) in enumerate(PANELS) for i in range(0, TILES, BANK // w)]
+        last = len(units) - 1
         sums, square, newacc, root = {}, {}, {}, {}
-        split = ("mom", len(units) - 1)
 
         def mx_pass(kind, s, j, g):
             c, i, n = units[s]
-            if g == 0 and (j == 0 or (kind, s) == split):
+            if g == 0 and (j == 0 or (kind, s) == ("mom", last)):
                 own = (4, 5) if kind == "grad" else (6, 7)
                 freed = (0, 1) if kind == "grad" else (2, 3)
                 bank = own[s % 2] if s < TILES else (freed + own)[(s + j) % 4]
-                sums[kind, s, j] = psum.tile([P, n, PANELS[c][1]], F32, name="bank%d" % bank)
-                for jj in range(j + 1, n):
-                    sums[kind, s, jj] = sums[kind, s, j]
+                tile = psum.tile([P, n, PANELS[c][1]], F32, name="bank%d" % bank)
+                for jj in range(j, n):
+                    sums[kind, s, jj] = tile
             nc.tensor.matmul_mx(
                 out=sums[kind, s, j][:, j, :],
                 lhsT=codes[kind, i + j][:, g * P : (g + 1) * P].bitcast(FP8X4),
@@ -199,89 +195,75 @@ def tile_eigenbasis_adagrad_step_d2_kernel(tc, mom_bytes, mom_scale, basis_bytes
                 for g in range(PASSES):
                     mx_pass(kind, s, j, g)
 
-        def out_view(rows, s):
+        def unit_view(rows, s):
             c, i, n = units[s]
             n0, w = PANELS[c]
             return rows[:, i : i + n, n0 : n0 + w]
 
-        def do_square(s):
+        def unit_tile(s, name, bufs):
             c, i, n = units[s]
-            square[s] = work.tile([P, n, PANELS[c][1]], F32, name="square", bufs=2)
+            return work.tile([P, n, PANELS[c][1]], F32, name=name, bufs=bufs)
+
+        def do_square(s):
+            square[s] = unit_tile(s, "square", 2)
             nc.scalar.activation(out=square[s][:], in_=sums["grad", s, 0][:], func=ACT.Square)
 
         def do_add(s):
-            c, i, n = units[s]
-            n0, w = PANELS[c]
-            newacc[s] = work.tile([P, n, w], F32, name="newacc", bufs=5)
-            nc.vector.tensor_tensor(out=newacc[s][:], in0=square[s][:], in1=accum_raw[:, i : i + n, n0 : n0 + w], op=ADD)
-            nc.sync.dma_start(out=out_view(newacc_rows, s), in_=newacc[s][:])
+            newacc[s] = unit_tile(s, "newacc", 5)
+            nc.vector.tensor_tensor(out=newacc[s][:], in0=square[s][:], in1=unit_view(accum_raw, s), op=ADD)
+            nc.sync.dma_start(out=unit_view(newacc_rows, s), in_=newacc[s][:])
 
         def do_root(s):
-            c, i, n = units[s]
-            root[s] = work.tile([P, n, PANELS[c][1]], F32, name="root", bufs=3)
+            root[s] = unit_tile(s, "root", 3)
             nc.scalar.activation(out=root[s][:], in_=newacc[s][:], func=ACT.Abs_reciprocal_sqrt)
 
         def do_step(s):
             c, i, n = units[s]
-            for js in [slice(j, j + 1) for j in range(n)] if ("mom", s) == split else [slice(0, n)]:
-                st = work.tile([P, js.stop - js.start, PANELS[c][1]], F32, name="step", bufs=5)
-                nc.vector.tensor_tensor(out=st[:], in0=sums["mom", s, js.start][:, js, :], in1=root[s][:, js, :], op=MULT)
-                nc.sync.dma_start(out=out_view(step_rows, s)[:, js, :], in_=st[:])
+            for js in [slice(j, j + 1) for j in range(n)] if s == last else [slice(0, n)]:
+                step = work.tile([P, js.stop - js.start, PANELS[c][1]], F32, name="step", bufs=5)
+                nc.vector.tensor_tensor(out=step[:], in0=sums["mom", s, js.start][:, js, :], in1=root[s][:, js, :], op=MULT)
+                nc.sync.dma_start(out=unit_view(step_rows, s)[:, js, :], in_=step[:])
 
+        first = [("grad", 0), ("mom", 0), ("grad", 1)]
+        scalar_pass = (1, 0)
         basis_widen(0, 0, 0, 2)
-        basis_widen(0, 0, 2, 4, True)
-        basis_widen(0, 1, 0, 4)
-        basis_interleave(0, 0)
-        turn("grad", 0)
-        mom_widen(0)
-        turn("mom", 0)
-        unload("grad", 0, 0)
-        basis_widen(0, 2, 0, 4)
-        unload("grad", 0, 1)
-        turn("grad", 1)
-        basis_quant(0, 0)
-        basis_interleave(0, 1)
-        basis_interleave(0, 2)
-        quant("grad", 0)
-        basis_quant(0, 1)
-        basis_quant(0, 2)
-        mx_pass("grad", 0, 0, 0)
-        mx_pass("grad", 0, 0, 1)
-        mx_pass("grad", 0, 0, 2)
-        basis_widen(0, 3, 0, 4)
-        unload("mom", 0, 0)
-        unload("mom", 0, 1)
-        turn("grad", 2)
-        unload("grad", 1, 0)
-        unload("grad", 1, 1)
-        unload("grad", 2, 0)
-        unload("grad", 2, 1)
-        mom_widen(1, 0, 8, True)
-        basis_interleave(0, 3)
-        quant("mom", 0)
-        mx_pass("mom", 0, 0, 0)
-        mx_pass("mom", 0, 0, 1)
-        mx_pass("mom", 0, 0, 2)
-        basis_quant(0, 3)
-        mx_pass("grad", 0, 0, 3)
-        mx_pass("mom", 0, 0, 3)
-        quant("grad", 1)
-        mom_widen(1, 8, 16, False)
-        quant("grad", 2)
+        basis_widen(0, 0, 2, 4, nc.vector.tensor_copy)
+        for g in range(PASSES):
+            basis_interleave(0, g)
+            if g == 0:
+                mom_widen(0, range(PASSES))
+            else:
+                quant(*first[g - 1])
+            basis_quant(0, g)
+            if g == 0:
+                turn(*first[0])
+                turn(*first[1])
+            else:
+                kind, i = first[g - 1]
+                for old in range(g):
+                    mx_pass(kind, i, 0, old)
+                for kind, i in first[:g]:
+                    mx_pass(kind, i, 0, g)
+            if g + 1 < PASSES:
+                basis_widen(0, g + 1, 0, 4)
+                unload(*first[g])
+                turn("grad", g + 1)
+        mom_widen(1, [scalar_pass[1]], on_scalar=True)
+        mom_widen(1, range(1, PASSES))
+        for i in range(2, GRAD_LEAD + 1):
+            unload("grad", i)
+            quant("grad", i)
 
-        later = [(c, g, t, t + BANK // w) for c, (n0, w) in enumerate(PANELS) if c > 0 for g in range(PASSES) for t in range(0, 4, BANK // w)]
-        quota = [1,1,1,1,1,1,2,3,3,2] + [0] * 16
-        share = [0,1,1,1,1] + [0] * 16
-        widened, shared = 0, 0
-        last = len(units) - 1
+        later = [(c, g, t) for c in (1, 2) for g in range(PASSES) for t in (0, 2)]
         for s in range(len(units)):
-            if 0 < s < TILES - 2:
-                turn("grad", s + 2)
+            grad_tile = s + GRAD_LEAD if 0 < s < TILES - GRAD_LEAD else None
+            if grad_tile:
+                turn("grad", grad_tile)
             if s > 0:
                 do_add(s)
             if 0 < s < TILES:
                 quant("mom", s)
-            if s + 1 < last:
+            if 0 < s < last - 1:
                 mx("grad", s + 1)
             if s + 2 == last:
                 mx("grad", last)
@@ -290,19 +272,16 @@ def tile_eigenbasis_adagrad_step_d2_kernel(tc, mom_bytes, mom_scale, basis_bytes
             if s > 0:
                 mx("mom", s)
 
-            ready = []
-            for c, g, t0, t1 in later[widened : widened + quota[s]]:
-                basis_widen(c, g, t0, t1)
-                widened = widened + 1
-                if t1 == 4:
-                    ready.append((c, g))
-            if 0 < s < TILES - 2:
-                unload("grad", s + 2, 0)
-                unload("grad", s + 2, 1)
+            now = later[sum(HALF_PASSES[:s]) : sum(HALF_PASSES[: s + 1])]
+            for c, g, t in now:
+                basis_widen(c, g, t, t + 2)
+            ready = [(c, g) for c, g, t in now if t == 2]
+            if grad_tile:
+                unload("grad", grad_tile)
             if s > 0:
                 do_step(s - 1)
             if s + 2 < TILES:
-                mom_widen(s + 2, sum(share) if s + 2 == 7 else 0)
+                mom_widen(s + 2, range(PASSES))
             if s == 0:
                 do_square(0)
                 do_add(0)
@@ -314,16 +293,12 @@ def tile_eigenbasis_adagrad_step_d2_kernel(tc, mom_bytes, mom_scale, basis_bytes
                 do_root(s)
             for c, g in ready:
                 basis_interleave(c, g)
-            if 0 < s < TILES - 2:
-                quant("grad", s + 2)
+            if grad_tile:
+                quant("grad", grad_tile)
             for c, g in ready:
                 basis_quant(c, g)
             if s + 1 < TILES:
-                unload("mom", s + 1, 0)
-                unload("mom", s + 1, 1)
+                unload("mom", s + 1)
             if s == 0:
                 do_root(0)
-            if share[s] > 0:
-                mom_widen(7, shared, shared + share[s], True)
-                shared = shared + share[s]
         do_step(last)

@@ -76,12 +76,13 @@ def tile_eigenbasis_adagrad_step_d2_kernel(tc, mom_bytes, mom_scale, basis_bytes
         load_grad(0)
         load_mom(0)
         load_basis(0, 2)
-        load_basis(0, 3)
         load_grad(1)
+        load_basis(0, 3)
+        load_grad(2)
         for i in range(1, TILES):
             load_mom(i)
-            if i + 1 < TILES:
-                load_grad(i + 1)
+            if i + 2 < TILES:
+                load_grad(i + 2)
             if i % 2 == 1:
                 load_accum(i // 2)
                 load_basis(1, i // 2)
@@ -149,7 +150,7 @@ def tile_eigenbasis_adagrad_step_d2_kernel(tc, mom_bytes, mom_scale, basis_bytes
                 for gg in range(2):
                     for u in range(2):
                         g = 2 * half + gg
-                        if kind == "mom" and (i, g) != scalar_pass:
+                        if kind == "mom" and (i == 0 or g > 0):
                             src = words[:, (2 * g + u) * P : (2 * g + u + 1) * P]
                         else:
                             src = words[:, 256 * g + u : 256 * (g + 1) : 2]
@@ -225,7 +226,6 @@ def tile_eigenbasis_adagrad_step_d2_kernel(tc, mom_bytes, mom_scale, basis_bytes
                 nc.sync.dma_start(out=unit_view(step_rows, s)[:, js, :], in_=step[:])
 
         first = [("grad", 0), ("mom", 0), ("grad", 1)]
-        scalar_pass = (1, 0)
         basis_widen(0, 0, 0, 2)
         basis_widen(0, 0, 2, 4, nc.vector.tensor_copy)
         for g in range(PASSES):
@@ -248,7 +248,7 @@ def tile_eigenbasis_adagrad_step_d2_kernel(tc, mom_bytes, mom_scale, basis_bytes
                 basis_widen(0, g + 1, 0, 4)
                 unload(*first[g])
                 turn("grad", g + 1)
-        mom_widen(1, [scalar_pass[1]], on_scalar=True)
+        mom_widen(1, [0], on_scalar=True)
         mom_widen(1, range(1, PASSES))
         for i in range(2, GRAD_LEAD + 1):
             unload("grad", i)
@@ -278,10 +278,8 @@ def tile_eigenbasis_adagrad_step_d2_kernel(tc, mom_bytes, mom_scale, basis_bytes
             ready = [(c, g) for c, g, t in now if t == 2]
             if grad_tile:
                 unload("grad", grad_tile)
-            if s > 0:
-                do_step(s - 1)
             if s + 2 < TILES:
-                mom_widen(s + 2, range(PASSES))
+                mom_widen(s + 2, range(1, PASSES))
             if s == 0:
                 do_square(0)
                 do_add(0)
@@ -293,6 +291,8 @@ def tile_eigenbasis_adagrad_step_d2_kernel(tc, mom_bytes, mom_scale, basis_bytes
                 do_root(s)
             for c, g in ready:
                 basis_interleave(c, g)
+            if s > 0:
+                do_step(s - 1)
             if grad_tile:
                 quant("grad", grad_tile)
             for c, g in ready:
@@ -301,4 +301,6 @@ def tile_eigenbasis_adagrad_step_d2_kernel(tc, mom_bytes, mom_scale, basis_bytes
                 unload("mom", s + 1)
             if s == 0:
                 do_root(0)
+            if s + 2 < TILES:
+                mom_widen(s + 2, [0], on_scalar=True)
         do_step(last)

@@ -42,14 +42,9 @@ def tile_eigenbasis_adagrad_step_d2_kernel(tc, mom_bytes, mom_scale, basis_bytes
 
         mom_sc = keep.tile([P, TILES, K // B], F32, name="mom_sc")
         basis_sc = keep.tile([P, PASSES, N // B], F32, name="basis_sc")
-        nc.scalar.dma_start(out=mom_sc[:], in_=mom_scale.rearrange("(p i) j -> p i j", i=TILES))
-        all_sc = keep.tile([P, PASSES, 4, N // B], F32, name="all_sc")
-        nc.scalar.dma_start(out=all_sc[:].rearrange("p g q b -> p (g q b)"), in_=basis_scale.rearrange("j b -> (j b)").partition_broadcast(P))
         warm = keep.tile([P, 2], F32, name="warm")
         nc.vector.memset(warm[:, 0:1], 1.0)
         nc.scalar.activation(out=warm[:, 1:2], in_=warm[:, 0:1], func=ACT.Abs_reciprocal_sqrt)
-        for q in range(4):
-            nc.vector.tensor_copy(out=basis_sc[32 * q : 32 * q + 32, :, :], in_=all_sc[32 * q : 32 * q + 32, :, q, :])
 
         basis_raw, mom_raw, grad_raw = {}, {}, {}
         accum_raw = keep.tile([P, TILES, N], BF16, name="accum_raw")
@@ -60,6 +55,14 @@ def tile_eigenbasis_adagrad_step_d2_kernel(tc, mom_bytes, mom_scale, basis_bytes
             for t0, t1 in ((0, 2), (2, 4)) if (c, g) == (0, 0) else ((0, 4),):
                 nc.sync.dma_start(out=basis_raw[c, g][:, t0:t1, :], in_=basis_rows[g][:, t0:t1, n0 : n0 + w])
 
+        def load_basis_scales():
+            by_quadrant = basis_scale.rearrange("(g q) b -> q g b", q=4)
+            for q in range(4):
+                nc.sync.dma_start(out=basis_sc[32 * q : 32 * q + 32, :, :], in_=by_quadrant[q].partition_broadcast(32))
+
+        def load_mom_scales():
+            nc.sync.dma_start(out=mom_sc[:], in_=mom_scale.rearrange("(p i) j -> p i j", i=TILES))
+
         def load_mom(i):
             mom_raw[i] = keep.tile([P, K], U8, name="mom_raw%d" % i)
             nc.sync.dma_start(out=mom_raw[i][:], in_=mom_rows[:, i, :])
@@ -68,26 +71,31 @@ def tile_eigenbasis_adagrad_step_d2_kernel(tc, mom_bytes, mom_scale, basis_bytes
             grad_raw[i] = keep.tile([P, K], BF16, name="grad_raw%d" % i)
             nc.sync.dma_start(out=grad_raw[i][:], in_=grad_rows[:, i, :])
 
-        def load_accum(j):
-            nc.sync.dma_start(out=accum_raw[:, 2 * j : 2 * j + 2, :], in_=accum_rows[:, 2 * j : 2 * j + 2, :])
+        def load_accum(tiles, cols):
+            nc.sync.dma_start(out=accum_raw[:, tiles, cols], in_=accum_rows[:, tiles, cols])
 
         load_basis(0, 0)
+        load_basis_scales()
         load_basis(0, 1)
         load_grad(0)
+        load_mom_scales()
         load_mom(0)
         load_basis(0, 2)
         load_grad(1)
         load_basis(0, 3)
         load_grad(2)
+        first_cols, later_cols = slice(0, PANELS[0][1]), slice(PANELS[0][1], N)
         for i in range(1, TILES):
             load_mom(i)
             if i + 2 < TILES:
                 load_grad(i + 2)
             if i % 2 == 1:
-                load_accum(i // 2)
+                load_accum(slice(i - 1, i + 1), first_cols)
                 load_basis(1, i // 2)
         for g in range(PASSES):
             load_basis(2, g)
+        for i in range(0, TILES, 4):
+            load_accum(slice(i, i + 4), later_cols)
 
         ident = keep.tile([P, P], F32, name="ident")
         make_identity(nc, ident[:])
@@ -150,7 +158,7 @@ def tile_eigenbasis_adagrad_step_d2_kernel(tc, mom_bytes, mom_scale, basis_bytes
                 for gg in range(2):
                     for u in range(2):
                         g = 2 * half + gg
-                        if kind == "mom" and (i == 0 or g > 0):
+                        if kind == "mom" and (i % 2 == 0 or g > 0):
                             src = words[:, (2 * g + u) * P : (2 * g + u + 1) * P]
                         else:
                             src = words[:, 256 * g + u : 256 * (g + 1) : 2]
@@ -279,7 +287,7 @@ def tile_eigenbasis_adagrad_step_d2_kernel(tc, mom_bytes, mom_scale, basis_bytes
             if grad_tile:
                 unload("grad", grad_tile)
             if s + 2 < TILES:
-                mom_widen(s + 2, range(1, PASSES))
+                mom_widen(s + 2, range(s % 2, PASSES))
             if s == 0:
                 do_square(0)
                 do_add(0)
@@ -301,6 +309,6 @@ def tile_eigenbasis_adagrad_step_d2_kernel(tc, mom_bytes, mom_scale, basis_bytes
                 unload("mom", s + 1)
             if s == 0:
                 do_root(0)
-            if s + 2 < TILES:
+            if s + 2 < TILES and s % 2 == 1:
                 mom_widen(s + 2, [0], on_scalar=True)
         do_step(last)

@@ -22,6 +22,7 @@ TILES = T // P
 BANK = 512
 PANELS = ((0, 512), (512, 256), (768, 256))
 GRAD_LEAD = 3
+LOAD_AHEAD = 3
 HALF_PASSES = (1, 1, 1, 1, 1, 1, 2, 3, 3, 2)
 
 
@@ -84,18 +85,24 @@ def tile_eigenbasis_adagrad_step_d2_kernel(tc, mom_bytes, mom_scale, basis_bytes
         load_grad(1)
         load_basis(0, 3)
         load_grad(2)
+        load_mom(1)
+        load_grad(3)
+        later = [(c, g, t) for c in (1, 2) for g in range(PASSES) for t in (0, 2)]
+        widened_in = [s for s, n in enumerate(HALF_PASSES) for repeat in range(n)]
         first_cols, later_cols = slice(0, PANELS[0][1]), slice(PANELS[0][1], N)
-        for i in range(1, TILES):
-            load_mom(i)
-            if i + 2 < TILES:
-                load_grad(i + 2)
-            if i % 2 == 1:
-                load_accum(slice(i - 1, i + 1), first_cols)
-                load_basis(1, i // 2)
-        for g in range(PASSES):
-            load_basis(2, g)
-        for i in range(0, TILES, 4):
-            load_accum(slice(i, i + 4), later_cols)
+        plan = [(i - GRAD_LEAD, load_grad, (i,)) for i in range(GRAD_LEAD + 1, TILES)]
+        plan = plan + [(i, load_accum, (slice(i, i + 2), first_cols)) for i in range(0, TILES, 2)]
+        plan = plan + [(s, load_basis, (c, g)) for s, (c, g, t) in zip(widened_in, later) if t == 0]
+        plan = plan + [(i - 2, load_mom, (i,)) for i in range(2, TILES)]
+        plan = plan + [(TILES + i // 2, load_accum, (slice(i, i + 4), later_cols)) for i in range(0, TILES, 4)]
+
+        def loads_for(s):
+            for need, load, args in plan:
+                if need == s:
+                    load(*args)
+
+        for s in range(LOAD_AHEAD + 1):
+            loads_for(s)
 
         ident = keep.tile([P, P], F32, name="ident")
         make_identity(nc, ident[:])
@@ -262,12 +269,13 @@ def tile_eigenbasis_adagrad_step_d2_kernel(tc, mom_bytes, mom_scale, basis_bytes
             unload("grad", i)
             quant("grad", i)
 
-        later = [(c, g, t) for c in (1, 2) for g in range(PASSES) for t in (0, 2)]
         for s in range(len(units)):
+            if s > 0:
+                loads_for(s + LOAD_AHEAD)
             grad_tile = s + GRAD_LEAD if 0 < s < TILES - GRAD_LEAD else None
             if grad_tile:
                 turn("grad", grad_tile)
-            if s > 0:
+            if 0 < s < last:
                 do_add(s)
             if 0 < s < TILES:
                 quant("mom", s)
@@ -295,8 +303,12 @@ def tile_eigenbasis_adagrad_step_d2_kernel(tc, mom_bytes, mom_scale, basis_bytes
                 do_root(s)
             if s < last:
                 do_square(s + 1)
-            if s >= TILES - 1:
+            if s + 1 == last:
+                do_add(last)
+            if TILES - 1 <= s < last:
                 do_root(s)
+            if s + 1 == last:
+                do_root(last)
             for c, g in ready:
                 basis_interleave(c, g)
             if s > 0:

@@ -56,10 +56,11 @@ def tile_eigenbasis_adagrad_step_d2_kernel(tc, mom_bytes, mom_scale, basis_bytes
             for t0, t1 in ((0, 2), (2, 4)) if (c, g) == (0, 0) else ((0, 4),):
                 nc.sync.dma_start(out=basis_raw[c, g][:, t0:t1, :], in_=basis_rows[g][:, t0:t1, n0 : n0 + w])
 
+        scale_rows = keep.tile([P, N // B], F32, name="scale_rows")
+        nc.vector.memset(scale_rows[:], 0.0)
+
         def load_basis_scales():
-            by_quadrant = basis_scale.rearrange("(g q) b -> q g b", q=4)
-            for q in range(4):
-                nc.sync.dma_start(out=basis_sc[32 * q : 32 * q + 32, :, :], in_=by_quadrant[q].partition_broadcast(32))
+            nc.sync.dma_start(out=scale_rows[0 : K // B, :], in_=basis_scale)
 
         def load_mom_scales():
             nc.sync.dma_start(out=mom_sc[:], in_=mom_scale.rearrange("(p i) j -> p i j", i=TILES))
@@ -107,6 +108,18 @@ def tile_eigenbasis_adagrad_step_d2_kernel(tc, mom_bytes, mom_scale, basis_bytes
         ident = keep.tile([P, P], F32, name="ident")
         make_identity(nc, ident[:])
 
+        def spread_turn(half):
+            bank = psum.tile([P, 4, P], F32, name="bank%d" % (5 + half))
+            for b in range(4):
+                column = scale_rows[:, 4 * half + b : 4 * half + b + 1]
+                nc.tensor.transpose(bank[:, b, :], column.to_broadcast([P, P]), ident[:])
+            return bank
+
+        def spread_pick(half, bank):
+            for q in range(4):
+                rows = slice(32 * q, 32 * q + 32)
+                nc.vector.tensor_copy(out=basis_sc[rows, :, 4 * half : 4 * half + 4], in_=bank[rows, :, q : K // B : 4].rearrange("p b g -> p g b"))
+
         basis_wide, basis_grp, basis_q, basis_qs = {}, {}, {}, {}
 
         def basis_widen(c, g, t0, t1, copy=nc.scalar.copy):
@@ -129,15 +142,15 @@ def tile_eigenbasis_adagrad_step_d2_kernel(tc, mom_bytes, mom_scale, basis_bytes
 
         def basis_quant(c, g):
             w = PANELS[c][1]
-            basis_q[c, g] = keep.tile([P, w], U32, name="basis_q%d%d" % (c, g), align_bytes=64)
-            basis_qs[c, g] = keep.tile([P, w], U8, name="basis_qs%d%d" % (c, g), align_bytes=64)
+            basis_q[c, g] = keep.tile([P, w], U32, name="basis_q%d%d" % (c, g), align_bytes=256)
+            basis_qs[c, g] = keep.tile([P, w], U8, name="basis_qs%d%d" % (c, g), align_bytes=256)
             nc.vector.quantize_mx(out=basis_q[c, g][:].bitcast(FP8X4), scales=basis_qs[c, g][:], in_=basis_grp[c, g][:].rearrange("p n t -> p (n t)"))
 
         mom_wide, turned, grouped, codes, scales = {}, {}, {}, {}, {}
 
         def mom_widen(i, passes, on_scalar=False):
             if i not in mom_wide:
-                mom_wide[i] = work.tile([P, PASSES, 2, P, 2], BF16, name="mom_wide", align_bytes=64, bufs=4)
+                mom_wide[i] = work.tile([P, PASSES, 2, P, 2], BF16, name="mom_wide", align_bytes=64, bufs=3)
             for g in passes:
                 for q in range(4):
                     j = 4 * g + q
@@ -179,8 +192,8 @@ def tile_eigenbasis_adagrad_step_d2_kernel(tc, mom_bytes, mom_scale, basis_bytes
                 nc.scalar.copy(out=words[:, 2 * half : 2 * half + 2, :, :], in_=turned[kind, i, half][:].rearrange("p g u r -> p g r u"))
 
         def quant(kind, i):
-            codes[kind, i] = keep.tile([P, PASSES * P], U32, name="%s_q%d" % (kind, i), align_bytes=64)
-            scales[kind, i] = keep.tile([P, PASSES * P], U8, name="%s_qs%d" % (kind, i), align_bytes=64)
+            codes[kind, i] = keep.tile([P, PASSES * P], U32, name="%s_q%d" % (kind, i), align_bytes=256)
+            scales[kind, i] = keep.tile([P, PASSES * P], U8, name="%s_qs%d" % (kind, i), align_bytes=256)
             nc.vector.quantize_mx(out=codes[kind, i][:].bitcast(FP8X4), scales=scales[kind, i][:], in_=grouped[kind, i][:].rearrange("p g r t -> p (g r t)"))
 
         units = [(c, i, BANK // w) for c, (n0, w) in enumerate(PANELS) for i in range(0, TILES, BANK // w)]
@@ -241,11 +254,14 @@ def tile_eigenbasis_adagrad_step_d2_kernel(tc, mom_bytes, mom_scale, basis_bytes
                 nc.sync.dma_start(out=unit_view(step_rows, s)[:, js, :], in_=step[:])
 
         first = [("grad", 0), ("mom", 0), ("grad", 1)]
+        spread_banks = [spread_turn(0), spread_turn(1)]
         basis_widen(0, 0, 0, 2)
         basis_widen(0, 0, 2, 4, nc.vector.tensor_copy)
+        spread_pick(0, spread_banks[0])
         for g in range(PASSES):
             basis_interleave(0, g)
             if g == 0:
+                spread_pick(1, spread_banks[1])
                 mom_widen(0, range(PASSES))
             else:
                 quant(*first[g - 1])
@@ -299,6 +315,8 @@ def tile_eigenbasis_adagrad_step_d2_kernel(tc, mom_bytes, mom_scale, basis_bytes
             if s == 0:
                 do_square(0)
                 do_add(0)
+            if s == 1:
+                do_root(0)
             if 0 < s < TILES - 1:
                 do_root(s)
             if s < last:
@@ -319,8 +337,6 @@ def tile_eigenbasis_adagrad_step_d2_kernel(tc, mom_bytes, mom_scale, basis_bytes
                 basis_quant(c, g)
             if s + 1 < TILES:
                 unload("mom", s + 1)
-            if s == 0:
-                do_root(0)
             if s + 2 < TILES and s % 2 == 1:
                 mom_widen(s + 2, [0], on_scalar=True)
         do_step(last)

@@ -20,10 +20,19 @@ P = 128
 PASSES = K // 512
 TILES = T // P
 BANK = 512
-PANELS = ((0, 512), (512, 256), (768, 256))
-GRAD_LEAD = 3
-LOAD_AHEAD = 3
-HALF_PASSES = (1, 1, 1, 1, 1, 1, 2, 3, 3, 2)
+PANEL = 256
+PANELS = N // PANEL
+GRAD_BUFS = 8
+ACC_BUFS = 8
+MOM_WIDE_BUFS = 16
+GROUPED_BUFS = 4
+ROOT_BUFS = 2
+STEP_BUFS = 3
+MS, MV = 2, 2
+
+
+def on_scalar(i, g):
+    return i >= 3 and g < 2
 
 
 def tile_eigenbasis_adagrad_step_d2_kernel(tc, mom_bytes, mom_scale, basis_bytes, basis_scale, grad, accum, out_0, out_1):
@@ -41,23 +50,18 @@ def tile_eigenbasis_adagrad_step_d2_kernel(tc, mom_bytes, mom_scale, basis_bytes
         newacc_rows = out_1.rearrange("(p i) n -> p i n", i=TILES)
         basis_rows = basis_bytes.rearrange("(g p t) n -> g p t n", p=P, t=4)
 
-        mom_sc = keep.tile([P, TILES, K // B], F32, name="mom_sc")
-        basis_sc = keep.tile([P, PASSES, N // B], F32, name="basis_sc")
         warm = keep.tile([P, 2], F32, name="warm")
         nc.vector.memset(warm[:, 0:1], 1.0)
         nc.scalar.activation(out=warm[:, 1:2], in_=warm[:, 0:1], func=ACT.Abs_reciprocal_sqrt)
 
-        basis_raw, mom_raw, grad_raw = {}, {}, {}
-        accum_raw = keep.tile([P, TILES, N], BF16, name="accum_raw")
-
-        def load_basis(c, g):
-            n0, w = PANELS[c]
-            basis_raw[c, g] = keep.tile([P, 4, w], U8, name="basis_raw%d%d" % (c, g))
-            for t0, t1 in ((0, 2), (2, 4)) if (c, g) == (0, 0) else ((0, 4),):
-                nc.sync.dma_start(out=basis_raw[c, g][:, t0:t1, :], in_=basis_rows[g][:, t0:t1, n0 : n0 + w])
-
+        basis_raw, mom_raw, grad_raw, accum_raw = {}, {}, {}, {}
+        mom_sc = keep.tile([P, TILES, K // B], F32, name="mom_sc")
         scale_rows = keep.tile([P, N // B], F32, name="scale_rows")
         nc.vector.memset(scale_rows[:], 0.0)
+
+        def load_basis(c, g):
+            basis_raw[c, g] = keep.tile([P, 4, PANEL], U8, name="basis_raw%d%d" % (c, g))
+            nc.sync.dma_start(out=basis_raw[c, g][:], in_=basis_rows[g][:, :, c * PANEL : (c + 1) * PANEL])
 
         def load_basis_scales():
             nc.sync.dma_start(out=scale_rows[0 : K // B, :], in_=basis_scale)
@@ -70,273 +74,249 @@ def tile_eigenbasis_adagrad_step_d2_kernel(tc, mom_bytes, mom_scale, basis_bytes
             nc.sync.dma_start(out=mom_raw[i][:], in_=mom_rows[:, i, :])
 
         def load_grad(i):
-            grad_raw[i] = keep.tile([P, K], BF16, name="grad_raw%d" % i)
+            grad_raw[i] = work.tile([P, K], BF16, name="grad_raw", bufs=GRAD_BUFS)
             nc.sync.dma_start(out=grad_raw[i][:], in_=grad_rows[:, i, :])
 
-        def load_accum(tiles, cols):
-            nc.sync.dma_start(out=accum_raw[:, tiles, cols], in_=accum_rows[:, tiles, cols])
-
-        load_basis(0, 0)
-        load_basis_scales()
-        load_basis(0, 1)
-        load_grad(0)
-        load_mom_scales()
-        load_mom(0)
-        load_basis(0, 2)
-        load_grad(1)
-        load_basis(0, 3)
-        load_grad(2)
-        load_mom(1)
-        load_grad(3)
-        later = [(c, g, t) for c in (1, 2) for g in range(PASSES) for t in (0, 2)]
-        widened_in = [s for s, n in enumerate(HALF_PASSES) for repeat in range(n)]
-        first_cols, later_cols = slice(0, PANELS[0][1]), slice(PANELS[0][1], N)
-        plan = [(i - GRAD_LEAD, load_grad, (i,)) for i in range(GRAD_LEAD + 1, TILES)]
-        plan = plan + [(i, load_accum, (slice(i, i + 2), first_cols)) for i in range(0, TILES, 2)]
-        plan = plan + [(s, load_basis, (c, g)) for s, (c, g, t) in zip(widened_in, later) if t == 0]
-        plan = plan + [(i - 2, load_mom, (i,)) for i in range(2, TILES)]
-        plan = plan + [(TILES + i // 2, load_accum, (slice(i, i + 4), later_cols)) for i in range(0, TILES, 4)]
-
-        def loads_for(s):
-            for need, load, args in plan:
-                if need == s:
-                    load(*args)
-
-        for s in range(LOAD_AHEAD + 1):
-            loads_for(s)
+        def load_accum(i):
+            accum_raw[i] = work.tile([P, N], BF16, name="accum_raw", bufs=ACC_BUFS)
+            nc.sync.dma_start(out=accum_raw[i][:], in_=accum_rows[:, i, :])
 
         ident = keep.tile([P, P], F32, name="ident")
-        make_identity(nc, ident[:])
+        pick = keep.tile([P, K // B, 32], F32, name="pick")
+        basis_sc = keep.tile([P, PASSES, N // B], F32, name="basis_sc")
 
-        def spread_turn(half):
-            bank = psum.tile([P, 4, P], F32, name="bank%d" % (5 + half))
-            for b in range(4):
-                column = scale_rows[:, 4 * half + b : 4 * half + b + 1]
-                nc.tensor.transpose(bank[:, b, :], column.to_broadcast([P, P]), ident[:])
+        def make_pick():
+            make_identity(nc, ident[:])
+            nc.vector.tensor_copy(out=pick[:], in_=ident[:, 0 : K // B].unsqueeze(2).to_broadcast([P, K // B, 32]))
+
+        def spread_scales():
+            bank = psum.tile([P, PASSES, N // B], F32, name="bank7")
+            for g in range(PASSES):
+                nc.tensor.matmul(bank[:, g, :], lhsT=pick[:, 4 * g : 4 * g + 4, :].rearrange("p q r -> p (q r)"), rhs=scale_rows[:], start=True, stop=True)
             return bank
 
-        def spread_pick(half, bank):
-            for q in range(4):
-                rows = slice(32 * q, 32 * q + 32)
-                nc.vector.tensor_copy(out=basis_sc[rows, :, 4 * half : 4 * half + 4], in_=bank[rows, :, q : K // B : 4].rearrange("p b g -> p g b"))
+        basis_wide, basis_grp = {}, {}
+        basis_q = [keep.tile([P, N], U32, name="basis_q%d" % g, align_bytes=256) for g in range(PASSES)]
+        basis_qs = [keep.tile([P, N], U8, name="basis_qs%d" % g, align_bytes=256) for g in range(PASSES)]
 
-        basis_wide, basis_grp, basis_q, basis_qs = {}, {}, {}, {}
-
-        def basis_widen(c, g, t0, t1, copy=nc.scalar.copy):
-            if t0 == 0:
-                basis_wide[c, g] = work.tile([P, 4, PANELS[c][1]], BF16, name="basis_wide", bufs=3)
-            copy(out=basis_wide[c, g][:, t0:t1, :], in_=basis_raw[c, g][:, t0:t1, :].bitcast(FP8))
+        def basis_widen(c, g, copy):
+            basis_wide[c, g] = work.tile([P, 4, PANEL], BF16, name="basis_wide", bufs=4)
+            copy(out=basis_wide[c, g][:], in_=basis_raw[c, g][:].bitcast(FP8))
 
         def basis_interleave(c, g):
-            n0, w = PANELS[c]
-            basis_grp[c, g] = work.tile([P, w, 4], BF16, name="basis_grp", align_bytes=64, bufs=3)
-            for b in range(w // B):
+            basis_grp[c, g] = work.tile([P, PANEL, 4], BF16, name="basis_grp", align_bytes=64, bufs=3)
+            for b in range(PANEL // B):
                 cols = slice(B * b, B * b + B)
+                block = c * PANEL // B + b
                 nc.vector.tensor_scalar(
                     out=basis_grp[c, g][:, cols, :].rearrange("p (c i) t -> p c t i", i=4),
                     in0=basis_wide[c, g][:, :, cols].rearrange("p t (c i) -> p c t i", i=4),
-                    scalar1=basis_sc[:, g, n0 // B + b : n0 // B + b + 1],
+                    scalar1=basis_sc[:, g, block : block + 1],
                     scalar2=None,
                     op0=MULT,
                 )
 
         def basis_quant(c, g):
-            w = PANELS[c][1]
-            basis_q[c, g] = keep.tile([P, w], U32, name="basis_q%d%d" % (c, g), align_bytes=256)
-            basis_qs[c, g] = keep.tile([P, w], U8, name="basis_qs%d%d" % (c, g), align_bytes=256)
-            nc.vector.quantize_mx(out=basis_q[c, g][:].bitcast(FP8X4), scales=basis_qs[c, g][:], in_=basis_grp[c, g][:].rearrange("p n t -> p (n t)"))
+            cols = slice(c * PANEL, (c + 1) * PANEL)
+            nc.vector.quantize_mx(out=basis_q[g][:, cols].bitcast(FP8X4), scales=basis_qs[g][:, cols], in_=basis_grp[c, g][:].rearrange("p n t -> p (n t)"))
 
         mom_wide, turned, grouped, codes, scales = {}, {}, {}, {}, {}
 
-        def mom_widen(i, passes, on_scalar=False):
-            if i not in mom_wide:
-                mom_wide[i] = work.tile([P, PASSES, 2, P, 2], BF16, name="mom_wide", align_bytes=64, bufs=3)
-            for g in passes:
-                for q in range(4):
-                    j = 4 * g + q
-                    src = mom_raw[i][:, B * j : B * j + B].bitcast(FP8)
-                    if on_scalar:
-                        dst = mom_wide[i][:].rearrange("p g u w e -> p (g u w e)")[:, B * j : B * j + B]
-                        nc.scalar.activation(out=dst, in_=src, func=ACT.Copy, scale=mom_sc[:, i, j : j + 1])
-                    else:
-                        nc.vector.tensor_scalar(
-                            out=mom_wide[i][:, g, :, 32 * q : 32 * q + 32, :].rearrange("p u w e -> p w u e"),
-                            in0=src.rearrange("p (w u e) -> p w u e", u=2, e=2),
-                            scalar1=mom_sc[:, i, j : j + 1],
-                            scalar2=None,
-                            op0=MULT,
-                        )
+        def mom_widen(i, g):
+            mom_wide[i, g] = work.tile([P, 512], BF16, name="mom_wide", align_bytes=64, bufs=MOM_WIDE_BUFS)
+            for q in range(4):
+                j = 4 * g + q
+                src = mom_raw[i][:, B * j : B * j + B].bitcast(FP8)
+                if on_scalar(i, g):
+                    nc.scalar.activation(out=mom_wide[i, g][:, B * q : B * q + B], in_=src, func=ACT.Copy, scale=mom_sc[:, i, j : j + 1])
+                else:
+                    nc.vector.tensor_scalar(
+                        out=mom_wide[i, g][:].rearrange("p (u w e) -> p w u e", u=2, e=2)[:, 32 * q : 32 * q + 32, :, :],
+                        in0=src.rearrange("p (w u e) -> p w u e", u=2, e=2),
+                        scalar1=mom_sc[:, i, j : j + 1],
+                        scalar2=None,
+                        op0=MULT,
+                    )
 
         def turn(kind, i):
-            if kind == "mom":
-                words = mom_wide[i][:].rearrange("p g u w e -> p (g u w e)").bitcast(F32)
-            else:
-                words = grad_raw[i][:].bitcast(F32)
-            turns = len(turned) // 2
+            pair = len(turned) // 2 % 2
             for half in range(2):
-                bank = psum.tile([P, 2, 2, P], F32, name="bank%d" % (2 * (turns % 2) + (half + turns // 2) % 2))
+                bank = psum.tile([P, 2, 2, P], F32, name="bank%d" % (2 * pair + half))
                 for gg in range(2):
+                    g = 2 * half + gg
                     for u in range(2):
-                        g = 2 * half + gg
-                        if kind == "mom" and (i % 2 == 0 or g > 0):
-                            src = words[:, (2 * g + u) * P : (2 * g + u + 1) * P]
+                        if kind == "grad":
+                            src = grad_raw[i][:].bitcast(F32)[:, 256 * g + u : 256 * (g + 1) : 2]
+                        elif on_scalar(i, g):
+                            src = mom_wide[i, g][:].bitcast(F32)[:, u : 256 : 2]
                         else:
-                            src = words[:, 256 * g + u : 256 * (g + 1) : 2]
+                            src = mom_wide[i, g][:].bitcast(F32)[:, u * P : (u + 1) * P]
                         nc.tensor.transpose(bank[:, gg, u, :], src, ident[:])
                 turned[kind, i, half] = bank
 
-        def unload(kind, i):
-            grouped[kind, i] = work.tile([P, PASSES, P, 4], BF16, name="grouped", align_bytes=64, bufs=5)
-            words = grouped[kind, i][:].rearrange("p g r t -> p (g r t)").bitcast(F32).rearrange("p (g r u) -> p g r u", r=P, u=2)
-            for half in range(2):
+        def unload(kind, i, halves=(0, 1)):
+            if 0 in halves:
+                grouped[kind, i] = work.tile([P, PASSES * P * 4], BF16, name="grouped", align_bytes=64, bufs=GROUPED_BUFS)
+            words = grouped[kind, i][:].bitcast(F32).rearrange("p (g r u) -> p g r u", r=P, u=2)
+            for half in halves:
                 nc.scalar.copy(out=words[:, 2 * half : 2 * half + 2, :, :], in_=turned[kind, i, half][:].rearrange("p g u r -> p g r u"))
 
         def quant(kind, i):
-            codes[kind, i] = keep.tile([P, PASSES * P], U32, name="%s_q%d" % (kind, i), align_bytes=256)
-            scales[kind, i] = keep.tile([P, PASSES * P], U8, name="%s_qs%d" % (kind, i), align_bytes=256)
-            nc.vector.quantize_mx(out=codes[kind, i][:].bitcast(FP8X4), scales=scales[kind, i][:], in_=grouped[kind, i][:].rearrange("p g r t -> p (g r t)"))
+            pool, name, bufs = (keep, "grad%d" % i, 1) if kind == "grad" else (work, "mom", 3)
+            codes[kind, i] = pool.tile([P, PASSES * P], U32, name=name + "_q", align_bytes=256, bufs=bufs)
+            scales[kind, i] = pool.tile([P, PASSES * P], U8, name=name + "_qs", align_bytes=256, bufs=bufs)
+            nc.vector.quantize_mx(out=codes[kind, i][:].bitcast(FP8X4), scales=scales[kind, i][:], in_=grouped[kind, i][:])
 
-        units = [(c, i, BANK // w) for c, (n0, w) in enumerate(PANELS) for i in range(0, TILES, BANK // w)]
-        last = len(units) - 1
-        sums, square, newacc, root = {}, {}, {}, {}
-
-        def mx_pass(kind, s, j, g):
-            c, i, n = units[s]
-            if g == 0 and (j == 0 or (kind, s) == ("mom", last)):
-                own = (4, 5) if kind == "grad" else (6, 7)
-                freed = (0, 1) if kind == "grad" else (2, 3)
-                bank = own[s % 2] if s < TILES else (freed + own)[(s + j) % 4]
-                tile = psum.tile([P, n, PANELS[c][1]], F32, name="bank%d" % bank)
-                for jj in range(j, n):
-                    sums[kind, s, jj] = tile
+        def mx_pass(out, kind, i, g, cols):
             nc.tensor.matmul_mx(
-                out=sums[kind, s, j][:, j, :],
-                lhsT=codes[kind, i + j][:, g * P : (g + 1) * P].bitcast(FP8X4),
-                lhsT_scale=scales[kind, i + j][:, g * P : (g + 1) * P],
-                rhs=basis_q[c, g][:].bitcast(FP8X4),
-                rhs_scale=basis_qs[c, g][:],
+                out=out,
+                lhsT=codes[kind, i][:, g * P : (g + 1) * P].bitcast(FP8X4),
+                lhsT_scale=scales[kind, i][:, g * P : (g + 1) * P],
+                rhs=basis_q[g][:, cols].bitcast(FP8X4),
+                rhs_scale=basis_qs[g][:, cols],
                 start=(g == 0),
                 stop=(g == PASSES - 1),
             )
 
-        def mx(kind, s):
-            for j in range(units[s][2]):
+        h_bank, r_bank, root = {}, {}, {}
+        newacc = keep.tile([P, TILES, N], F32, name="newacc")
+
+        def h_sum(c, i, passes=range(PASSES)):
+            if (c, i // 2) not in h_bank:
+                h_bank[c, i // 2] = psum.tile([P, 2, PANEL], F32, name="bank%d" % ((0 if c == 2 else 4) + len(h_bank) % 4))
+            for g in passes:
+                mx_pass(h_bank[c, i // 2][:, i % 2, :], "grad", i, g, slice(c * PANEL, (c + 1) * PANEL))
+
+        def square(c, pair):
+            nc.scalar.activation(out=newacc[:, 2 * pair : 2 * pair + 2, c * PANEL : (c + 1) * PANEL], in_=h_bank[c, pair][:], func=ACT.Square)
+
+        def add(i):
+            nc.vector.tensor_tensor(out=newacc[:, i, :], in0=newacc[:, i, :], in1=accum_raw[i][:], op=ADD)
+            nc.sync.dma_start(out=newacc_rows[:, i, :], in_=newacc[:, i, :])
+
+        def take_root(i):
+            root[i] = work.tile([P, N], F32, name="root", bufs=ROOT_BUFS)
+            nc.scalar.activation(out=root[i][:], in_=newacc[:, i, :], func=ACT.Abs_reciprocal_sqrt)
+
+        def r_parts(i):
+            return [slice(0, 512), slice(512, 768), slice(768, 1024)] if i == TILES - 1 else [slice(0, 512), slice(512, 1024)]
+
+        def r_sum(i):
+            for cols in r_parts(i):
+                r_bank[i, cols.start] = psum.tile([P, cols.stop - cols.start], F32, name="bank%d" % (4 + len(r_bank) % 4))
                 for g in range(PASSES):
-                    mx_pass(kind, s, j, g)
+                    mx_pass(r_bank[i, cols.start][:], "mom", i, g, cols)
 
-        def unit_view(rows, s):
-            c, i, n = units[s]
-            n0, w = PANELS[c]
-            return rows[:, i : i + n, n0 : n0 + w]
+        def step(i):
+            out = work.tile([P, N], F32, name="step", bufs=STEP_BUFS)
+            for cols in r_parts(i):
+                nc.vector.tensor_tensor(out=out[:, cols], in0=r_bank[i, cols.start][:], in1=root[i][:, cols], op=MULT)
+                nc.sync.dma_start(out=step_rows[:, i, cols], in_=out[:, cols])
 
-        def unit_tile(s, name, bufs):
-            c, i, n = units[s]
-            return work.tile([P, n, PANELS[c][1]], F32, name=name, bufs=bufs)
+        on_vector, on_act = nc.vector.tensor_copy, nc.scalar.copy
+        load_basis_scales()
+        for g in range(4):
+            load_basis(0, g)
+        for i in range(3):
+            load_grad(i)
+        load_basis(1, 0)
+        load_basis(1, 1)
+        load_grad(3)
+        load_basis(1, 2)
+        load_basis(1, 3)
+        for i in range(4, 7):
+            load_grad(i)
+        for g in range(4):
+            load_basis(2, g)
+        load_grad(7)
+        load_mom_scales()
+        load_mom(0)
+        for g in range(4):
+            load_basis(3, g)
+        for i in range(TILES):
+            if i + 1 < TILES:
+                load_mom(i + 1)
+            load_accum(i)
+        make_pick()
+        bank = spread_scales()
+        mw = [(i, g) for i in range(TILES) for g in range(PASSES) if not on_scalar(i, g)]
+        ms = [(i, g) for i in range(TILES) for g in range(PASSES) if on_scalar(i, g)]
+        def m(lst, n):
+            for r in range(n):
+                if lst: mom_widen(*lst.pop(0))
+        H = lambda c, *tiles: [h_sum(c, i) for i in tiles]
+        def TG(i):
+            turn("grad", i)
+        U = lambda i: unload("grad", i)
+        qg = lambda i: quant("grad", i)
+        W = basis_widen
+        slots = {
+            (0, 0): lambda: (nc.vector.tensor_copy(out=basis_sc[:], in_=bank[:]), W(0, 2, on_act), W(0, 3, on_act)),
+            (0, 1): lambda: (TG(0), U(0), TG(1)),
+            (0, 2): lambda: (U(1), TG(2)),
+            (0, 3): lambda: (qg(0), U(2)),
+            (1, 0): lambda: (H(0, 0), TG(3), qg(1), H(0, 1), W(1, 2, on_act), U(3), TG(4)),
+            (1, 1): lambda: (qg(2), H(0, 2), W(1, 3, on_act), U(4), TG(5)),
+            (1, 2): lambda: (qg(3), H(0, 3), U(5), TG(6)),
+            (1, 3): lambda: (qg(4), square(0, 0), U(6)),
+            (2, 0): lambda: (H(1, 0, 1), TG(7), qg(5), H(0, 4, 5), W(2, 2, on_act), square(0, 1), U(7)),
+            (2, 1): lambda: (qg(6), H(1, 2, 3), W(2, 3, on_act), square(1, 0)),
+            (2, 2): lambda: (qg(7), m(mw, 1), H(0, 6, 7), square(0, 2), H(1, 4, 5), square(1, 1)),
+            (2, 3): lambda: (m(mw, 1), H(1, 6, 7)),
+            (3, 0): lambda: (W(3, 2, on_act), square(0, 3), H(2, 0, 1, 2, 3)),
+            (3, 1): lambda: (m(mw, 1), W(3, 3, on_act), square(1, 2), square(1, 3), H(2, 4, 5, 6, 7)),
+            (3, 2): lambda: (square(2, 0), square(2, 1)),
+            (3, 3): lambda: (m(ms, 1)),
+        }
+        for c in range(PANELS):
+            W(c, 0, on_vector)
+            slots[c, 0]()
+            W(c, 1, on_vector)
+            basis_interleave(c, 0)
+            slots[c, 1]()
+            basis_interleave(c, 1)
+            basis_quant(c, 0)
+            basis_interleave(c, 2)
+            basis_quant(c, 1)
+            slots[c, 2]()
+            basis_interleave(c, 3)
+            basis_quant(c, 2)
+            slots[c, 3]()
+            basis_quant(c, 3)
 
-        def do_square(s):
-            square[s] = unit_tile(s, "square", 2)
-            nc.scalar.activation(out=square[s][:], in_=sums["grad", s, 0][:], func=ACT.Square)
+        H(3, 0, 1, 2, 3)
+        square(2, 2)
+        m(ms, 1)
+        square(2, 3)
+        m(mw, 5)
+        turn("mom", 0)
 
-        def do_add(s):
-            newacc[s] = unit_tile(s, "newacc", 5)
-            nc.vector.tensor_tensor(out=newacc[s][:], in0=square[s][:], in1=unit_view(accum_raw, s), op=ADD)
-            nc.sync.dma_start(out=unit_view(newacc_rows, s), in_=newacc[s][:])
-
-        def do_root(s):
-            root[s] = unit_tile(s, "root", 3)
-            nc.scalar.activation(out=root[s][:], in_=newacc[s][:], func=ACT.Abs_reciprocal_sqrt)
-
-        def do_step(s):
-            c, i, n = units[s]
-            for js in [slice(j, j + 1) for j in range(n)] if s == last else [slice(0, n)]:
-                step = work.tile([P, js.stop - js.start, PANELS[c][1]], F32, name="step", bufs=5)
-                nc.vector.tensor_tensor(out=step[:], in0=sums["mom", s, js.start][:, js, :], in1=root[s][:, js, :], op=MULT)
-                nc.sync.dma_start(out=unit_view(step_rows, s)[:, js, :], in_=step[:])
-
-        first = [("grad", 0), ("mom", 0), ("grad", 1)]
-        spread_banks = [spread_turn(0), spread_turn(1)]
-        basis_widen(0, 0, 0, 2)
-        basis_widen(0, 0, 2, 4, nc.vector.tensor_copy)
-        spread_pick(0, spread_banks[0])
-        for g in range(PASSES):
-            basis_interleave(0, g)
-            if g == 0:
-                spread_pick(1, spread_banks[1])
-                mom_widen(0, range(PASSES))
-            else:
-                quant(*first[g - 1])
-            basis_quant(0, g)
-            if g == 0:
-                turn(*first[0])
-                turn(*first[1])
-            else:
-                kind, i = first[g - 1]
-                for old in range(g):
-                    mx_pass(kind, i, 0, old)
-                for kind, i in first[:g]:
-                    mx_pass(kind, i, 0, g)
-            if g + 1 < PASSES:
-                basis_widen(0, g + 1, 0, 4)
-                unload(*first[g])
-                turn("grad", g + 1)
-        mom_widen(1, [0], on_scalar=True)
-        mom_widen(1, range(1, PASSES))
-        for i in range(2, GRAD_LEAD + 1):
-            unload("grad", i)
-            quant("grad", i)
-
-        for s in range(len(units)):
-            if s > 0:
-                loads_for(s + LOAD_AHEAD)
-            grad_tile = s + GRAD_LEAD if 0 < s < TILES - GRAD_LEAD else None
-            if grad_tile:
-                turn("grad", grad_tile)
-            if 0 < s < last:
-                do_add(s)
-            if 0 < s < TILES:
-                quant("mom", s)
-            if 0 < s < last - 1:
-                mx("grad", s + 1)
-            if s + 2 == last:
-                mx("grad", last)
-            if s + 1 < TILES:
-                turn("mom", s + 1)
-            if s > 0:
-                mx("mom", s)
-
-            now = later[sum(HALF_PASSES[:s]) : sum(HALF_PASSES[: s + 1])]
-            for c, g, t in now:
-                basis_widen(c, g, t, t + 2)
-            ready = [(c, g) for c, g, t in now if t == 2]
-            if grad_tile:
-                unload("grad", grad_tile)
-            if s + 2 < TILES:
-                mom_widen(s + 2, range(s % 2, PASSES))
-            if s == 0:
-                do_square(0)
-                do_add(0)
-            if s == 1:
-                do_root(0)
-            if 0 < s < TILES - 1:
-                do_root(s)
-            if s < last:
-                do_square(s + 1)
-            if s + 1 == last:
-                do_add(last)
-            if TILES - 1 <= s < last:
-                do_root(s)
-            if s + 1 == last:
-                do_root(last)
-            for c, g in ready:
-                basis_interleave(c, g)
-            if s > 0:
-                do_step(s - 1)
-            if grad_tile:
-                quant("grad", grad_tile)
-            for c, g in ready:
-                basis_quant(c, g)
-            if s + 1 < TILES:
-                unload("mom", s + 1)
-            if s + 2 < TILES and s % 2 == 1:
-                mom_widen(s + 2, [0], on_scalar=True)
-        do_step(last)
+        square(3, 0)
+        H(3, 4, 5)
+        unload("mom", 0)
+        square(3, 1)
+        H(3, 6, 7)
+        m(mw, 4)
+        turn("mom", 1)
+        add(0)
+        quant("mom", 0)
+        square(3, 2)
+        square(3, 3)
+        add(1)
+        m(mw, 2)
+        for i in range(TILES):
+            r_sum(i)
+            if i + 1 < TILES:
+                unload("mom", i + 1)
+            if i > 0:
+                step(i - 1)
+            if i + 1 < TILES:
+                quant("mom", i + 1)
+            if i + 2 < TILES:
+                add(i + 2)
+            take_root(i)
+            m(ms, MS)
+            m(mw, MV)
+            if i + 2 < TILES:
+                turn("mom", i + 2)
+        step(TILES - 1)

@@ -32,7 +32,7 @@ MS, MV = 2, 2
 
 
 def on_scalar(i, g):
-    return i >= 3 and g < 2
+    return (i >= 2 and g < 2)
 
 
 def tile_eigenbasis_adagrad_step_d2_kernel(tc, mom_bytes, mom_scale, basis_bytes, basis_scale, grad, accum, out_0, out_1):
@@ -57,7 +57,7 @@ def tile_eigenbasis_adagrad_step_d2_kernel(tc, mom_bytes, mom_scale, basis_bytes
         basis_raw, mom_raw, grad_raw, accum_raw = {}, {}, {}, {}
         mom_sc = keep.tile([P, TILES, K // B], F32, name="mom_sc")
         scale_rows = keep.tile([P, N // B], F32, name="scale_rows")
-        nc.vector.memset(scale_rows[:], 0.0)
+        nc.gpsimd.memset(scale_rows[:], 0.0)
 
         def load_basis(c, g):
             basis_raw[c, g] = keep.tile([P, 4, PANEL], U8, name="basis_raw%d%d" % (c, g))
@@ -215,24 +215,32 @@ def tile_eigenbasis_adagrad_step_d2_kernel(tc, mom_bytes, mom_scale, basis_bytes
 
         on_vector, on_act = nc.vector.tensor_copy, nc.scalar.copy
         load_basis_scales()
-        for g in range(4):
-            load_basis(0, g)
-        for i in range(3):
-            load_grad(i)
+        load_basis(0, 0)
+        load_basis(0, 1)
+        load_basis(0, 2)
+        load_grad(0)
+        load_basis(0, 3)
+        load_grad(1)
+        load_grad(2)
         load_basis(1, 0)
         load_basis(1, 1)
         load_grad(3)
         load_basis(1, 2)
         load_basis(1, 3)
-        for i in range(4, 7):
-            load_grad(i)
-        for g in range(4):
-            load_basis(2, g)
+        load_grad(4)
+        load_grad(5)
+        load_grad(6)
+        load_basis(2, 0)
+        load_basis(2, 1)
+        load_basis(2, 2)
+        load_basis(2, 3)
         load_grad(7)
         load_mom_scales()
         load_mom(0)
-        for g in range(4):
-            load_basis(3, g)
+        load_basis(3, 0)
+        load_basis(3, 1)
+        load_basis(3, 2)
+        load_basis(3, 3)
         for i in range(TILES):
             if i + 1 < TILES:
                 load_mom(i + 1)
@@ -251,7 +259,7 @@ def tile_eigenbasis_adagrad_step_d2_kernel(tc, mom_bytes, mom_scale, basis_bytes
         qg = lambda i: quant("grad", i)
         W = basis_widen
         slots = {
-            (0, 0): lambda: (nc.vector.tensor_copy(out=basis_sc[:], in_=bank[:]), W(0, 2, on_act), W(0, 3, on_act)),
+            (0, 0): lambda: (nc.vector.tensor_copy(out=basis_sc[:], in_=bank[:]), W(0, 1, on_act), W(0, 2, on_act), W(0, 3, on_act)),
             (0, 1): lambda: (TG(0), U(0), TG(1)),
             (0, 2): lambda: (U(1), TG(2)),
             (0, 3): lambda: (qg(0), U(2)),
@@ -271,7 +279,8 @@ def tile_eigenbasis_adagrad_step_d2_kernel(tc, mom_bytes, mom_scale, basis_bytes
         for c in range(PANELS):
             W(c, 0, on_vector)
             slots[c, 0]()
-            W(c, 1, on_vector)
+            if c > 0:
+                W(c, 1, on_vector)
             basis_interleave(c, 0)
             slots[c, 1]()
             basis_interleave(c, 1)
@@ -288,22 +297,22 @@ def tile_eigenbasis_adagrad_step_d2_kernel(tc, mom_bytes, mom_scale, basis_bytes
         square(2, 2)
         m(ms, 1)
         square(2, 3)
-        m(mw, 5)
+        m(mw, 4)
         turn("mom", 0)
-
         square(3, 0)
+        m(ms, 1)
         H(3, 4, 5)
         unload("mom", 0)
         square(3, 1)
         H(3, 6, 7)
-        m(mw, 4)
+        m(mw, 3)
         turn("mom", 1)
         add(0)
         quant("mom", 0)
         square(3, 2)
         square(3, 3)
         add(1)
-        m(mw, 2)
+        m(mw, 3)
         for i in range(TILES):
             r_sum(i)
             if i + 1 < TILES:

@@ -22,17 +22,11 @@ TILES = T // P
 BANK = 512
 PANEL = 256
 PANELS = N // PANEL
-GRAD_BUFS = 8
-ACC_BUFS = 8
-MOM_WIDE_BUFS = 16
-GROUPED_BUFS = 4
-ROOT_BUFS = 2
-STEP_BUFS = 3
-MS, MV = 2, 2
+MOM_WIDE_BUFS = 4 * PASSES
 
 
 def on_scalar(i, g):
-    return (i >= 2 and g < 2)
+    return i >= 2 and g < 2
 
 
 def tile_eigenbasis_adagrad_step_d2_kernel(tc, mom_bytes, mom_scale, basis_bytes, basis_scale, grad, accum, out_0, out_1):
@@ -74,22 +68,20 @@ def tile_eigenbasis_adagrad_step_d2_kernel(tc, mom_bytes, mom_scale, basis_bytes
             nc.sync.dma_start(out=mom_raw[i][:], in_=mom_rows[:, i, :])
 
         def load_grad(i):
-            grad_raw[i] = work.tile([P, K], BF16, name="grad_raw", bufs=GRAD_BUFS)
+            grad_raw[i] = work.tile([P, K], BF16, name="grad_raw", bufs=TILES)
             nc.sync.dma_start(out=grad_raw[i][:], in_=grad_rows[:, i, :])
 
         def load_accum(i):
-            accum_raw[i] = work.tile([P, N], BF16, name="accum_raw", bufs=ACC_BUFS)
+            accum_raw[i] = work.tile([P, N], BF16, name="accum_raw", bufs=TILES)
             nc.sync.dma_start(out=accum_raw[i][:], in_=accum_rows[:, i, :])
 
         ident = keep.tile([P, P], F32, name="ident")
         pick = keep.tile([P, K // B, 32], F32, name="pick")
         basis_sc = keep.tile([P, PASSES, N // B], F32, name="basis_sc")
 
-        def make_pick():
+        def spread_scales():
             make_identity(nc, ident[:])
             nc.vector.tensor_copy(out=pick[:], in_=ident[:, 0 : K // B].unsqueeze(2).to_broadcast([P, K // B, 32]))
-
-        def spread_scales():
             bank = psum.tile([P, PASSES, N // B], F32, name="bank7")
             for g in range(PASSES):
                 nc.tensor.matmul(bank[:, g, :], lhsT=pick[:, 4 * g : 4 * g + 4, :].rearrange("p q r -> p (q r)"), rhs=scale_rows[:], start=True, stop=True)
@@ -154,11 +146,10 @@ def tile_eigenbasis_adagrad_step_d2_kernel(tc, mom_bytes, mom_scale, basis_bytes
                         nc.tensor.transpose(bank[:, gg, u, :], src, ident[:])
                 turned[kind, i, half] = bank
 
-        def unload(kind, i, halves=(0, 1)):
-            if 0 in halves:
-                grouped[kind, i] = work.tile([P, PASSES * P * 4], BF16, name="grouped", align_bytes=64, bufs=GROUPED_BUFS)
+        def unload(kind, i):
+            grouped[kind, i] = work.tile([P, PASSES * P * 4], BF16, name="grouped", align_bytes=64, bufs=4)
             words = grouped[kind, i][:].bitcast(F32).rearrange("p (g r u) -> p g r u", r=P, u=2)
-            for half in halves:
+            for half in range(2):
                 nc.scalar.copy(out=words[:, 2 * half : 2 * half + 2, :, :], in_=turned[kind, i, half][:].rearrange("p g u r -> p g r u"))
 
         def quant(kind, i):
@@ -181,11 +172,12 @@ def tile_eigenbasis_adagrad_step_d2_kernel(tc, mom_bytes, mom_scale, basis_bytes
         h_bank, r_bank, root = {}, {}, {}
         newacc = keep.tile([P, TILES, N], F32, name="newacc")
 
-        def h_sum(c, i, passes=range(PASSES)):
-            if (c, i // 2) not in h_bank:
-                h_bank[c, i // 2] = psum.tile([P, 2, PANEL], F32, name="bank%d" % ((0 if c == 2 else 4) + len(h_bank) % 4))
-            for g in passes:
-                mx_pass(h_bank[c, i // 2][:, i % 2, :], "grad", i, g, slice(c * PANEL, (c + 1) * PANEL))
+        def h_sums(c, *tiles):
+            for i in tiles:
+                if i % 2 == 0:
+                    h_bank[c, i // 2] = psum.tile([P, 2, PANEL], F32, name="bank%d" % ((0 if c == 2 else 4) + len(h_bank) % 4))
+                for g in range(PASSES):
+                    mx_pass(h_bank[c, i // 2][:, i % 2, :], "grad", i, g, slice(c * PANEL, (c + 1) * PANEL))
 
         def square(c, pair):
             nc.scalar.activation(out=newacc[:, 2 * pair : 2 * pair + 2, c * PANEL : (c + 1) * PANEL], in_=h_bank[c, pair][:], func=ACT.Square)
@@ -195,7 +187,7 @@ def tile_eigenbasis_adagrad_step_d2_kernel(tc, mom_bytes, mom_scale, basis_bytes
             nc.sync.dma_start(out=newacc_rows[:, i, :], in_=newacc[:, i, :])
 
         def take_root(i):
-            root[i] = work.tile([P, N], F32, name="root", bufs=ROOT_BUFS)
+            root[i] = work.tile([P, N], F32, name="root", bufs=2)
             nc.scalar.activation(out=root[i][:], in_=newacc[:, i, :], func=ACT.Abs_reciprocal_sqrt)
 
         def r_parts(i):
@@ -208,16 +200,14 @@ def tile_eigenbasis_adagrad_step_d2_kernel(tc, mom_bytes, mom_scale, basis_bytes
                     mx_pass(r_bank[i, cols.start][:], "mom", i, g, cols)
 
         def step(i):
-            out = work.tile([P, N], F32, name="step", bufs=STEP_BUFS)
+            out = work.tile([P, N], F32, name="step", bufs=3)
             for cols in r_parts(i):
                 nc.vector.tensor_tensor(out=out[:, cols], in0=r_bank[i, cols.start][:], in1=root[i][:, cols], op=MULT)
                 nc.sync.dma_start(out=step_rows[:, i, cols], in_=out[:, cols])
 
-        on_vector, on_act = nc.vector.tensor_copy, nc.scalar.copy
         load_basis_scales()
-        load_basis(0, 0)
-        load_basis(0, 1)
-        load_basis(0, 2)
+        for g in range(3):
+            load_basis(0, g)
         load_grad(0)
         load_basis(0, 3)
         load_grad(1)
@@ -227,105 +217,160 @@ def tile_eigenbasis_adagrad_step_d2_kernel(tc, mom_bytes, mom_scale, basis_bytes
         load_grad(3)
         load_basis(1, 2)
         load_basis(1, 3)
-        load_grad(4)
-        load_grad(5)
-        load_grad(6)
-        load_basis(2, 0)
-        load_basis(2, 1)
-        load_basis(2, 2)
-        load_basis(2, 3)
+        for i in range(4, 7):
+            load_grad(i)
+        for g in range(PASSES):
+            load_basis(2, g)
         load_grad(7)
         load_mom_scales()
         load_mom(0)
-        load_basis(3, 0)
-        load_basis(3, 1)
-        load_basis(3, 2)
-        load_basis(3, 3)
+        for g in range(PASSES):
+            load_basis(3, g)
         for i in range(TILES):
             if i + 1 < TILES:
                 load_mom(i + 1)
             load_accum(i)
-        make_pick()
-        bank = spread_scales()
-        mw = [(i, g) for i in range(TILES) for g in range(PASSES) if not on_scalar(i, g)]
-        ms = [(i, g) for i in range(TILES) for g in range(PASSES) if on_scalar(i, g)]
-        def m(lst, n):
-            for r in range(n):
-                if lst: mom_widen(*lst.pop(0))
-        H = lambda c, *tiles: [h_sum(c, i) for i in tiles]
-        def TG(i):
-            turn("grad", i)
-        U = lambda i: unload("grad", i)
-        qg = lambda i: quant("grad", i)
-        W = basis_widen
-        slots = {
-            (0, 0): lambda: (nc.vector.tensor_copy(out=basis_sc[:], in_=bank[:]), W(0, 1, on_act), W(0, 2, on_act), W(0, 3, on_act)),
-            (0, 1): lambda: (TG(0), U(0), TG(1)),
-            (0, 2): lambda: (U(1), TG(2)),
-            (0, 3): lambda: (qg(0), U(2)),
-            (1, 0): lambda: (H(0, 0), TG(3), qg(1), H(0, 1), W(1, 2, on_act), U(3), TG(4)),
-            (1, 1): lambda: (qg(2), H(0, 2), W(1, 3, on_act), U(4), TG(5)),
-            (1, 2): lambda: (qg(3), H(0, 3), U(5), TG(6)),
-            (1, 3): lambda: (qg(4), square(0, 0), U(6)),
-            (2, 0): lambda: (H(1, 0, 1), TG(7), qg(5), H(0, 4, 5), W(2, 2, on_act), square(0, 1), U(7)),
-            (2, 1): lambda: (qg(6), H(1, 2, 3), W(2, 3, on_act), square(1, 0)),
-            (2, 2): lambda: (qg(7), m(mw, 1), H(0, 6, 7), square(0, 2), H(1, 4, 5), square(1, 1)),
-            (2, 3): lambda: (m(mw, 1), H(1, 6, 7)),
-            (3, 0): lambda: (W(3, 2, on_act), square(0, 3), H(2, 0, 1, 2, 3)),
-            (3, 1): lambda: (m(mw, 1), W(3, 3, on_act), square(1, 2), square(1, 3), H(2, 4, 5, 6, 7)),
-            (3, 2): lambda: (square(2, 0), square(2, 1)),
-            (3, 3): lambda: (m(ms, 1)),
+        scales_bank = spread_scales()
+
+        todo = {
+            "vector": [(i, g) for i in range(TILES) for g in range(PASSES) if not on_scalar(i, g)],
+            "scalar": [(i, g) for i in range(TILES) for g in range(PASSES) if on_scalar(i, g)],
         }
+
+        def widen_next(engine, count):
+            for i, g in todo[engine][:count]:
+                mom_widen(i, g)
+            todo[engine] = todo[engine][count:]
+
+        def beside(n):
+            if n == 0:
+                nc.vector.tensor_copy(out=basis_sc[:], in_=scales_bank[:])
+                for g in range(1, PASSES):
+                    basis_widen(0, g, nc.scalar.copy)
+            elif n == 1:
+                turn("grad", 0)
+                unload("grad", 0)
+                turn("grad", 1)
+            elif n == 2:
+                unload("grad", 1)
+                turn("grad", 2)
+            elif n == 3:
+                quant("grad", 0)
+                unload("grad", 2)
+            elif n == 4:
+                h_sums(0, 0)
+                turn("grad", 3)
+                quant("grad", 1)
+                h_sums(0, 1)
+                basis_widen(1, 2, nc.scalar.copy)
+                unload("grad", 3)
+                turn("grad", 4)
+            elif n == 5:
+                quant("grad", 2)
+                h_sums(0, 2)
+                basis_widen(1, 3, nc.scalar.copy)
+                unload("grad", 4)
+                turn("grad", 5)
+            elif n == 6:
+                quant("grad", 3)
+                h_sums(0, 3)
+                unload("grad", 5)
+                turn("grad", 6)
+            elif n == 7:
+                quant("grad", 4)
+                square(0, 0)
+                unload("grad", 6)
+            elif n == 8:
+                h_sums(1, 0, 1)
+                turn("grad", 7)
+                quant("grad", 5)
+                h_sums(0, 4, 5)
+                basis_widen(2, 2, nc.scalar.copy)
+                square(0, 1)
+                unload("grad", 7)
+            elif n == 9:
+                quant("grad", 6)
+                h_sums(1, 2, 3)
+                basis_widen(2, 3, nc.scalar.copy)
+                square(1, 0)
+            elif n == 10:
+                quant("grad", 7)
+                widen_next("vector", 1)
+                h_sums(0, 6, 7)
+                square(0, 2)
+                h_sums(1, 4, 5)
+                square(1, 1)
+            elif n == 11:
+                widen_next("vector", 1)
+                h_sums(1, 6, 7)
+            elif n == 12:
+                basis_widen(3, 2, nc.scalar.copy)
+                square(0, 3)
+                h_sums(2, 0, 1, 2, 3)
+            elif n == 13:
+                widen_next("vector", 1)
+                basis_widen(3, 3, nc.scalar.copy)
+                square(1, 2)
+                square(1, 3)
+                h_sums(2, 4, 5, 6, 7)
+            elif n == 14:
+                square(2, 0)
+                square(2, 1)
+            else:
+                widen_next("scalar", 1)
+
         for c in range(PANELS):
-            W(c, 0, on_vector)
-            slots[c, 0]()
+            basis_widen(c, 0, nc.vector.tensor_copy)
+            beside(4 * c)
             if c > 0:
-                W(c, 1, on_vector)
+                basis_widen(c, 1, nc.vector.tensor_copy)
             basis_interleave(c, 0)
-            slots[c, 1]()
+            beside(4 * c + 1)
             basis_interleave(c, 1)
             basis_quant(c, 0)
             basis_interleave(c, 2)
             basis_quant(c, 1)
-            slots[c, 2]()
+            beside(4 * c + 2)
             basis_interleave(c, 3)
             basis_quant(c, 2)
-            slots[c, 3]()
+            beside(4 * c + 3)
             basis_quant(c, 3)
 
-        H(3, 0, 1, 2, 3)
+        h_sums(3, 0, 1, 2, 3)
         square(2, 2)
-        m(ms, 1)
+        widen_next("scalar", 1)
         square(2, 3)
-        m(mw, 4)
+        widen_next("vector", 5)
         turn("mom", 0)
-        square(3, 0)
-        m(ms, 1)
-        H(3, 4, 5)
-        unload("mom", 0)
-        square(3, 1)
-        H(3, 6, 7)
-        m(mw, 3)
         turn("mom", 1)
+        square(3, 0)
+        widen_next("scalar", 1)
+        h_sums(3, 4, 5, 6, 7)
+        widen_next("vector", 2)
+        unload("mom", 0)
+        unload("mom", 1)
         add(0)
+        widen_next("vector", 2)
         quant("mom", 0)
-        square(3, 2)
-        square(3, 3)
         add(1)
-        m(mw, 3)
+        quant("mom", 1)
+        for pair in range(1, 4):
+            square(3, pair)
+        widen_next("vector", 2)
+
         for i in range(TILES):
             r_sum(i)
-            if i + 1 < TILES:
+            if 0 < i < TILES - 1:
                 unload("mom", i + 1)
             if i > 0:
                 step(i - 1)
-            if i + 1 < TILES:
+            if 0 < i < TILES - 1:
                 quant("mom", i + 1)
             if i + 2 < TILES:
                 add(i + 2)
+            widen_next("scalar", 2 - i % 2)
             take_root(i)
-            m(ms, MS)
-            m(mw, MV)
+            widen_next("vector", 2 if i == 0 else 1)
             if i + 2 < TILES:
                 turn("mom", i + 2)
         step(TILES - 1)

@@ -19,10 +19,15 @@ ACT = mybir.ActivationFunctionType
 P = 128
 PASSES = K // 512
 TILES = T // P
-BANK = 512
 PANEL = 256
 PANELS = N // PANEL
 MOM_WIDE_BUFS = 4 * PASSES
+BASIS_WIDE_BUFS = PASSES
+BASIS_GRP_BUFS = 3
+GROUPED_BUFS = 4
+MOM_CODE_BUFS = 3
+ROOT_BUFS = 2
+STEP_BUFS = 3
 
 
 def on_scalar(i, g):
@@ -92,17 +97,17 @@ def tile_eigenbasis_adagrad_step_d2_kernel(tc, mom_bytes, mom_scale, basis_bytes
         basis_qs = [keep.tile([P, N], U8, name="basis_qs%d" % g, align_bytes=256) for g in range(PASSES)]
 
         def basis_widen(c, g, copy):
-            basis_wide[c, g] = work.tile([P, 4, PANEL], BF16, name="basis_wide", bufs=4)
+            basis_wide[c, g] = work.tile([P, 4, PANEL], BF16, name="basis_wide", bufs=BASIS_WIDE_BUFS)
             copy(out=basis_wide[c, g][:], in_=basis_raw[c, g][:].bitcast(FP8))
 
         def basis_interleave(c, g):
-            basis_grp[c, g] = work.tile([P, PANEL, 4], BF16, name="basis_grp", align_bytes=64, bufs=3)
+            basis_grp[c, g] = work.tile([P, PANEL, 4], BF16, name="basis_grp", align_bytes=64, bufs=BASIS_GRP_BUFS)
             for b in range(PANEL // B):
                 cols = slice(B * b, B * b + B)
                 block = c * PANEL // B + b
                 nc.vector.tensor_scalar(
-                    out=basis_grp[c, g][:, cols, :].rearrange("p (c i) t -> p c t i", i=4),
-                    in0=basis_wide[c, g][:, :, cols].rearrange("p t (c i) -> p c t i", i=4),
+                    out=basis_grp[c, g][:, cols, :].rearrange("p (m e) t -> p m t e", e=8),
+                    in0=basis_wide[c, g][:, :, cols].rearrange("p t (m e) -> p m t e", e=8),
                     scalar1=basis_sc[:, g, block : block + 1],
                     scalar2=None,
                     op0=MULT,
@@ -131,9 +136,9 @@ def tile_eigenbasis_adagrad_step_d2_kernel(tc, mom_bytes, mom_scale, basis_bytes
                     )
 
         def turn(kind, i):
-            pair = len(turned) // 2 % 2
+            first_bank = len(turned) % 4
             for half in range(2):
-                bank = psum.tile([P, 2, 2, P], F32, name="bank%d" % (2 * pair + half))
+                bank = psum.tile([P, 2, 2, P], F32, name="bank%d" % (first_bank + half))
                 for gg in range(2):
                     g = 2 * half + gg
                     for u in range(2):
@@ -147,13 +152,13 @@ def tile_eigenbasis_adagrad_step_d2_kernel(tc, mom_bytes, mom_scale, basis_bytes
                 turned[kind, i, half] = bank
 
         def unload(kind, i):
-            grouped[kind, i] = work.tile([P, PASSES * P * 4], BF16, name="grouped", align_bytes=64, bufs=4)
+            grouped[kind, i] = work.tile([P, PASSES * P * 4], BF16, name="grouped", align_bytes=64, bufs=GROUPED_BUFS)
             words = grouped[kind, i][:].bitcast(F32).rearrange("p (g r u) -> p g r u", r=P, u=2)
             for half in range(2):
                 nc.scalar.copy(out=words[:, 2 * half : 2 * half + 2, :, :], in_=turned[kind, i, half][:].rearrange("p g u r -> p g r u"))
 
         def quant(kind, i):
-            pool, name, bufs = (keep, "grad%d" % i, 1) if kind == "grad" else (work, "mom", 3)
+            pool, name, bufs = (keep, "grad%d" % i, 1) if kind == "grad" else (work, "mom", MOM_CODE_BUFS)
             codes[kind, i] = pool.tile([P, PASSES * P], U32, name=name + "_q", align_bytes=256, bufs=bufs)
             scales[kind, i] = pool.tile([P, PASSES * P], U8, name=name + "_qs", align_bytes=256, bufs=bufs)
             nc.vector.quantize_mx(out=codes[kind, i][:].bitcast(FP8X4), scales=scales[kind, i][:], in_=grouped[kind, i][:])
@@ -187,7 +192,7 @@ def tile_eigenbasis_adagrad_step_d2_kernel(tc, mom_bytes, mom_scale, basis_bytes
             nc.sync.dma_start(out=newacc_rows[:, i, :], in_=newacc[:, i, :])
 
         def take_root(i):
-            root[i] = work.tile([P, N], F32, name="root", bufs=2)
+            root[i] = work.tile([P, N], F32, name="root", bufs=ROOT_BUFS)
             nc.scalar.activation(out=root[i][:], in_=newacc[:, i, :], func=ACT.Abs_reciprocal_sqrt)
 
         def r_parts(i):
@@ -200,7 +205,7 @@ def tile_eigenbasis_adagrad_step_d2_kernel(tc, mom_bytes, mom_scale, basis_bytes
                     mx_pass(r_bank[i, cols.start][:], "mom", i, g, cols)
 
         def step(i):
-            out = work.tile([P, N], F32, name="step", bufs=3)
+            out = work.tile([P, N], F32, name="step", bufs=STEP_BUFS)
             for cols in r_parts(i):
                 nc.vector.tensor_tensor(out=out[:, cols], in0=r_bank[i, cols.start][:], in1=root[i][:, cols], op=MULT)
                 nc.sync.dma_start(out=step_rows[:, i, cols], in_=out[:, cols])
@@ -368,9 +373,10 @@ def tile_eigenbasis_adagrad_step_d2_kernel(tc, mom_bytes, mom_scale, basis_bytes
                 quant("mom", i + 1)
             if i + 2 < TILES:
                 add(i + 2)
-            widen_next("scalar", 2 - i % 2)
+                widen_next("scalar", 2 - i % 2)
             take_root(i)
-            widen_next("vector", 2 if i == 0 else 1)
+            if todo["vector"]:
+                widen_next("vector", 2 if i == 0 else 1)
             if i + 2 < TILES:
                 turn("mom", i + 2)
         step(TILES - 1)

from contextlib import ExitStack

import concourse.mybir as mybir
from concourse.masks import make_identity

T, K, N, B = 1024, 2048, 1024, 128
FLOPS = 2 * 2 * T * K * N

F32 = mybir.dt.float32
BF16 = mybir.dt.bfloat16
U32 = mybir.dt.uint32
U8 = mybir.dt.uint8
FP8 = mybir.dt.float8_e4m3fn
FP8X4 = mybir.dt.float8_e4m3fn_x4
MULT = mybir.AluOpType.mult
ADD = mybir.AluOpType.add
ACT = mybir.ActivationFunctionType

P = 128
PASSES = K // 512
TILES = T // P
PANEL = 256
PANELS = N // PANEL
MOM_WIDE_BUFS = 4 * PASSES
BASIS_WIDE_BUFS = PASSES
BASIS_GRP_BUFS = 3
GROUPED_BUFS = 4
MOM_CODE_BUFS = 3
ROOT_BUFS = 2
STEP_BUFS = 3


def on_scalar(i, g):
    return i >= 2 and g < 2


def tile_eigenbasis_adagrad_step_d2_kernel(tc, mom_bytes, mom_scale, basis_bytes, basis_scale, grad, accum, out_0, out_1):
    nc = tc.nc
    with ExitStack() as ctx:
        keep = ctx.enter_context(tc.tile_pool(name="keep", bufs=1))
        work = ctx.enter_context(tc.tile_pool(name="work", bufs=3))
        psum = ctx.enter_context(tc.psum_pool(name="psum", bufs=1))
        ctx.enter_context(tc.manual_schedule())

        mom_rows = mom_bytes.rearrange("(p i) k -> p i k", i=TILES)
        grad_rows = grad.rearrange("(p i) k -> p i k", i=TILES)
        accum_rows = accum.rearrange("(p i) n -> p i n", i=TILES)
        step_rows = out_0.rearrange("(p i) n -> p i n", i=TILES)
        newacc_rows = out_1.rearrange("(p i) n -> p i n", i=TILES)
        basis_rows = basis_bytes.rearrange("(g p t) n -> g p t n", p=P, t=4)

        warm = keep.tile([P, 2], F32, name="warm")
        nc.vector.memset(warm[:, 0:1], 1.0)
        nc.scalar.activation(out=warm[:, 1:2], in_=warm[:, 0:1], func=ACT.Abs_reciprocal_sqrt)

        basis_raw, mom_raw, grad_raw, accum_raw = {}, {}, {}, {}
        mom_sc = keep.tile([P, TILES, K // B], F32, name="mom_sc")
        scale_rows = keep.tile([P, N // B], F32, name="scale_rows")
        nc.gpsimd.memset(scale_rows[:], 0.0)

        def load_basis(c, g):
            basis_raw[c, g] = keep.tile([P, 4, PANEL], U8, name="basis_raw%d%d" % (c, g))
            nc.sync.dma_start(out=basis_raw[c, g][:], in_=basis_rows[g][:, :, c * PANEL : (c + 1) * PANEL])

        def load_basis_scales():
            nc.sync.dma_start(out=scale_rows[0 : K // B, :], in_=basis_scale)

        def load_mom_scales():
            nc.sync.dma_start(out=mom_sc[:], in_=mom_scale.rearrange("(p i) j -> p i j", i=TILES))

        def load_mom(i):
            mom_raw[i] = keep.tile([P, K], U8, name="mom_raw%d" % i)
            nc.sync.dma_start(out=mom_raw[i][:], in_=mom_rows[:, i, :])

        def load_grad(i):
            grad_raw[i] = work.tile([P, K], BF16, name="grad_raw", bufs=TILES)
            nc.sync.dma_start(out=grad_raw[i][:], in_=grad_rows[:, i, :])

        def load_accum(i):
            accum_raw[i] = work.tile([P, N], BF16, name="accum_raw", bufs=TILES)
            nc.sync.dma_start(out=accum_raw[i][:], in_=accum_rows[:, i, :])

        ident = keep.tile([P, P], F32, name="ident")
        pick = keep.tile([P, K // B, 32], F32, name="pick")
        basis_sc = keep.tile([P, PASSES, N // B], F32, name="basis_sc")

        def spread_scales():
            make_identity(nc, ident[:])
            nc.vector.tensor_copy(out=pick[:], in_=ident[:, 0 : K // B].unsqueeze(2).to_broadcast([P, K // B, 32]))
            bank = psum.tile([P, PASSES, N // B], F32, name="bank7")
            for g in range(PASSES):
                nc.tensor.matmul(bank[:, g, :], lhsT=pick[:, 4 * g : 4 * g + 4, :].rearrange("p q r -> p (q r)"), rhs=scale_rows[:], start=True, stop=True)
            return bank

        basis_wide, basis_grp = {}, {}
        basis_q = [keep.tile([P, N], U32, name="basis_q%d" % g, align_bytes=256) for g in range(PASSES)]
        basis_qs = [keep.tile([P, N], U8, name="basis_qs%d" % g, align_bytes=256) for g in range(PASSES)]

        def basis_widen(c, g, copy):
            basis_wide[c, g] = work.tile([P, 4, PANEL], BF16, name="basis_wide", bufs=BASIS_WIDE_BUFS)
            copy(out=basis_wide[c, g][:], in_=basis_raw[c, g][:].bitcast(FP8))

        def basis_interleave(c, g):
            basis_grp[c, g] = work.tile([P, PANEL, 4], BF16, name="basis_grp", align_bytes=64, bufs=BASIS_GRP_BUFS)
            for b in range(PANEL // B):
                cols = slice(B * b, B * b + B)
                block = c * PANEL // B + b
                nc.vector.tensor_scalar(
                    out=basis_grp[c, g][:, cols, :].rearrange("p (m e) t -> p m t e", e=8),
                    in0=basis_wide[c, g][:, :, cols].rearrange("p t (m e) -> p m t e", e=8),
                    scalar1=basis_sc[:, g, block : block + 1],
                    scalar2=None,
                    op0=MULT,
                )

        def basis_quant(c, g):
            cols = slice(c * PANEL, (c + 1) * PANEL)
            nc.vector.quantize_mx(out=basis_q[g][:, cols].bitcast(FP8X4), scales=basis_qs[g][:, cols], in_=basis_grp[c, g][:].rearrange("p n t -> p (n t)"))

        mom_wide, turned, grouped, codes, scales = {}, {}, {}, {}, {}

        def mom_widen(i, g):
            mom_wide[i, g] = work.tile([P, 512], BF16, name="mom_wide", align_bytes=64, bufs=MOM_WIDE_BUFS)
            for q in range(4):
                j = 4 * g + q
                src = mom_raw[i][:, B * j : B * j + B].bitcast(FP8)
                if on_scalar(i, g):
                    nc.scalar.activation(out=mom_wide[i, g][:, B * q : B * q + B], in_=src, func=ACT.Copy, scale=mom_sc[:, i, j : j + 1])
                else:
                    nc.vector.tensor_scalar(
                        out=mom_wide[i, g][:].rearrange("p (u w e) -> p w u e", u=2, e=2)[:, 32 * q : 32 * q + 32, :, :],
                        in0=src.rearrange("p (w u e) -> p w u e", u=2, e=2),
                        scalar1=mom_sc[:, i, j : j + 1],
                        scalar2=None,
                        op0=MULT,
                    )

        def turn(kind, i):
            first_bank = len(turned) % 4
            for half in range(2):
                bank = psum.tile([P, 2, 2, P], F32, name="bank%d" % (first_bank + half))
                for gg in range(2):
                    g = 2 * half + gg
                    for u in range(2):
                        if kind == "grad":
                            src = grad_raw[i][:].bitcast(F32)[:, 256 * g + u : 256 * (g + 1) : 2]
                        elif on_scalar(i, g):
                            src = mom_wide[i, g][:].bitcast(F32)[:, u : 256 : 2]
                        else:
                            src = mom_wide[i, g][:].bitcast(F32)[:, u * P : (u + 1) * P]
                        nc.tensor.transpose(bank[:, gg, u, :], src, ident[:])
                turned[kind, i, half] = bank

        def unload(kind, i):
            grouped[kind, i] = work.tile([P, PASSES * P * 4], BF16, name="grouped", align_bytes=64, bufs=GROUPED_BUFS)
            words = grouped[kind, i][:].bitcast(F32).rearrange("p (g r u) -> p g r u", r=P, u=2)
            for half in range(2):
                nc.scalar.copy(out=words[:, 2 * half : 2 * half + 2, :, :], in_=turned[kind, i, half][:].rearrange("p g u r -> p g r u"))

        def quant(kind, i):
            pool, name, bufs = (keep, "grad%d" % i, 1) if kind == "grad" else (work, "mom", MOM_CODE_BUFS)
            codes[kind, i] = pool.tile([P, PASSES * P], U32, name=name + "_q", align_bytes=256, bufs=bufs)
            scales[kind, i] = pool.tile([P, PASSES * P], U8, name=name + "_qs", align_bytes=256, bufs=bufs)
            nc.vector.quantize_mx(out=codes[kind, i][:].bitcast(FP8X4), scales=scales[kind, i][:], in_=grouped[kind, i][:])

        def mx_pass(out, kind, i, g, cols):
            nc.tensor.matmul_mx(
                out=out,
                lhsT=codes[kind, i][:, g * P : (g + 1) * P].bitcast(FP8X4),
                lhsT_scale=scales[kind, i][:, g * P : (g + 1) * P],
                rhs=basis_q[g][:, cols].bitcast(FP8X4),
                rhs_scale=basis_qs[g][:, cols],
                start=(g == 0),
                stop=(g == PASSES - 1),
            )

        h_bank, r_bank, root = {}, {}, {}
        newacc = keep.tile([P, TILES, N], F32, name="newacc")

        def h_sums(c, *tiles):
            for i in tiles:
                if i % 2 == 0:
                    h_bank[c, i // 2] = psum.tile([P, 2, PANEL], F32, name="bank%d" % ((0 if c == 2 else 4) + len(h_bank) % 4))
                for g in range(PASSES):
                    mx_pass(h_bank[c, i // 2][:, i % 2, :], "grad", i, g, slice(c * PANEL, (c + 1) * PANEL))

        def square(c, pair):
            nc.scalar.activation(out=newacc[:, 2 * pair : 2 * pair + 2, c * PANEL : (c + 1) * PANEL], in_=h_bank[c, pair][:], func=ACT.Square)

        def add(i):
            nc.vector.tensor_tensor(out=newacc[:, i, :], in0=newacc[:, i, :], in1=accum_raw[i][:], op=ADD)
            nc.sync.dma_start(out=newacc_rows[:, i, :], in_=newacc[:, i, :])

        def take_root(i):
            root[i] = work.tile([P, N], F32, name="root", bufs=ROOT_BUFS)
            nc.scalar.activation(out=root[i][:], in_=newacc[:, i, :], func=ACT.Abs_reciprocal_sqrt)

        def r_parts(i):
            return [slice(0, 512), slice(512, 768), slice(768, 1024)] if i == TILES - 1 else [slice(0, 512), slice(512, 1024)]

        def r_sum(i):
            for cols in r_parts(i):
                r_bank[i, cols.start] = psum.tile([P, cols.stop - cols.start], F32, name="bank%d" % (4 + len(r_bank) % 4))
                for g in range(PASSES):
                    mx_pass(r_bank[i, cols.start][:], "mom", i, g, cols)

        def step(i):
            out = work.tile([P, N], F32, name="step", bufs=STEP_BUFS)
            for cols in r_parts(i):
                nc.vector.tensor_tensor(out=out[:, cols], in0=r_bank[i, cols.start][:], in1=root[i][:, cols], op=MULT)
                nc.sync.dma_start(out=step_rows[:, i, cols], in_=out[:, cols])

        load_basis_scales()
        for g in range(3):
            load_basis(0, g)
        load_grad(0)
        load_basis(0, 3)
        load_grad(1)
        load_grad(2)
        load_basis(1, 0)
        load_basis(1, 1)
        load_grad(3)
        load_basis(1, 2)
        load_basis(1, 3)
        for i in range(4, 7):
            load_grad(i)
        for g in range(PASSES):
            load_basis(2, g)
        load_grad(7)
        load_mom_scales()
        load_mom(0)
        for g in range(PASSES):
            load_basis(3, g)
        for i in range(TILES):
            if i + 1 < TILES:
                load_mom(i + 1)
            load_accum(i)
        scales_bank = spread_scales()

        todo = {
            "vector": [(i, g) for i in range(TILES) for g in range(PASSES) if not on_scalar(i, g)],
            "scalar": [(i, g) for i in range(TILES) for g in range(PASSES) if on_scalar(i, g)],
        }

        def widen_next(engine, count):
            for i, g in todo[engine][:count]:
                mom_widen(i, g)
            todo[engine] = todo[engine][count:]

        def beside(n):
            if n == 0:
                nc.vector.tensor_copy(out=basis_sc[:], in_=scales_bank[:])
                for g in range(1, PASSES):
                    basis_widen(0, g, nc.scalar.copy)
            elif n == 1:
                turn("grad", 0)
                unload("grad", 0)
                turn("grad", 1)
            elif n == 2:
                unload("grad", 1)
                turn("grad", 2)
            elif n == 3:
                quant("grad", 0)
                unload("grad", 2)
            elif n == 4:
                h_sums(0, 0)
                turn("grad", 3)
                quant("grad", 1)
                h_sums(0, 1)
                basis_widen(1, 2, nc.scalar.copy)
                unload("grad", 3)
                turn("grad", 4)
            elif n == 5:
                quant("grad", 2)
                h_sums(0, 2)
                basis_widen(1, 3, nc.scalar.copy)
                unload("grad", 4)
                turn("grad", 5)
            elif n == 6:
                quant("grad", 3)
                h_sums(0, 3)
                unload("grad", 5)
                turn("grad", 6)
            elif n == 7:
                quant("grad", 4)
                square(0, 0)
                unload("grad", 6)
            elif n == 8:
                h_sums(1, 0, 1)
                turn("grad", 7)
                quant("grad", 5)
                h_sums(0, 4, 5)
                basis_widen(2, 2, nc.scalar.copy)
                square(0, 1)
                unload("grad", 7)
            elif n == 9:
                quant("grad", 6)
                h_sums(1, 2, 3)
                basis_widen(2, 3, nc.scalar.copy)
                square(1, 0)
            elif n == 10:
                quant("grad", 7)
                widen_next("vector", 1)
                h_sums(0, 6, 7)
                square(0, 2)
                h_sums(1, 4, 5)
                square(1, 1)
            elif n == 11:
                widen_next("vector", 1)
                h_sums(1, 6, 7)
            elif n == 12:
                basis_widen(3, 2, nc.scalar.copy)
                square(0, 3)
                h_sums(2, 0, 1, 2, 3)
            elif n == 13:
                widen_next("vector", 1)
                basis_widen(3, 3, nc.scalar.copy)
                square(1, 2)
                square(1, 3)
                h_sums(2, 4, 5, 6, 7)
            elif n == 14:
                square(2, 0)
                square(2, 1)
            else:
                widen_next("scalar", 1)

        for c in range(PANELS):
            basis_widen(c, 0, nc.vector.tensor_copy)
            beside(4 * c)
            if c > 0:
                basis_widen(c, 1, nc.vector.tensor_copy)
            basis_interleave(c, 0)
            beside(4 * c + 1)
            basis_interleave(c, 1)
            basis_quant(c, 0)
            basis_interleave(c, 2)
            basis_quant(c, 1)
            beside(4 * c + 2)
            basis_interleave(c, 3)
            basis_quant(c, 2)
            beside(4 * c + 3)
            basis_quant(c, 3)

        h_sums(3, 0, 1, 2, 3)
        square(2, 2)
        widen_next("scalar", 1)
        square(2, 3)
        widen_next("vector", 5)
        turn("mom", 0)
        turn("mom", 1)
        square(3, 0)
        widen_next("scalar", 1)
        h_sums(3, 4, 5, 6, 7)
        widen_next("vector", 2)
        unload("mom", 0)
        unload("mom", 1)
        add(0)
        widen_next("vector", 2)
        quant("mom", 0)
        add(1)
        quant("mom", 1)
        for pair in range(1, 4):
            square(3, pair)
        widen_next("vector", 2)

        for i in range(TILES):
            r_sum(i)
            if 0 < i < TILES - 1:
                unload("mom", i + 1)
            if i > 0:
                step(i - 1)
            if 0 < i < TILES - 1:
                quant("mom", i + 1)
            if i + 2 < TILES:
                add(i + 2)
                widen_next("scalar", 2 - i % 2)
            take_root(i)
            if todo["vector"]:
                widen_next("vector", 2 if i == 0 else 1)
            if i + 2 < TILES:
                turn("mom", i + 2)
        step(TILES - 1)
